import numpy as np
import ml_dtypes


def mxq(x, axis, fmt="e4m3"):
    dtype, down = {"e4m3": (ml_dtypes.float8_e4m3fn, 7), "e5m2": (ml_dtypes.float8_e5m2, 14)}[fmt]
    v = np.moveaxis(np.asarray(x, np.float32).astype(ml_dtypes.bfloat16).astype(np.float64), axis, -1)
    blocks = v.reshape(v.shape[:-1] + (-1, 32))
    amax = np.abs(blocks).max(-1, keepdims=True)
    byte = np.maximum(np.where(amax > 0, np.frexp(amax)[1] - 1 + 127, 0) - down, 1)
    scale = np.exp2(byte - 127.0)
    codes = (blocks / scale).astype(np.float32).astype(dtype).astype(np.float64)
    return np.moveaxis((codes * scale).reshape(v.shape), -1, axis)


WIDE = False


def mx_kscale(k):
    if not WIDE:
        return np.ones(k)
    levels = np.array([10, -10, 5, -5, 0])
    if k % 512:
        return np.exp2(np.random.permutation(np.resize(levels, k // 32))).repeat(32)
    a = np.empty((k // 512, 16))
    for p in range(k // 512):
        a[p, :8] = np.random.permutation(np.resize(levels, 8))
        for g in range(8):
            far = levels[np.abs(levels - a[p, g]) >= 10]
            a[p, g + 8] = far[np.random.randint(len(far))]
    return np.exp2(a.ravel()).repeat(32)


def f64(x):
    return np.asarray(x).astype(np.float64)


def striped(idx):
    return np.tile(np.asarray(idx).reshape(-1, 16).T, (8, 1)).astype(np.uint16)


def unstriped(offs):
    return offs[:16].T.reshape(-1).astype(np.int64)


E2M1 = np.array([0.0, 0.5, 1.0, 1.5, 2.0, 3.0, 4.0, 6.0, -0.0, -0.5, -1.0, -1.5, -2.0, -3.0, -4.0, -6.0])


def pack_weight(w, fmt):
    k, n = w.shape
    w = f64(np.asarray(w, np.float32).astype(ml_dtypes.bfloat16)).reshape(k // 32, 32, n)
    amax = np.abs(w).max(1)
    if fmt == "e4m3":
        byte = np.frexp(amax)[1] - 1 + 127 - 7
    else:
        mant, ex = np.frexp(amax / 6.0)
        byte = np.where(mant > 0.5, ex, ex - 1) + 127
    byte = np.clip(np.where(amax > 0, byte, 1), 1, 254)
    scaled = (w * np.exp2(127.0 - byte)[:, None, :]).reshape(k, n).astype(np.float32)
    by_word = np.ascontiguousarray(scaled.reshape(k // 512, 128, 4, n).transpose(0, 1, 3, 2))
    if fmt == "e4m3":
        words = by_word.astype(ml_dtypes.float8_e4m3fn).view(np.uint8)
    else:
        c = by_word.astype(ml_dtypes.float4_e2m1fn).view(np.uint8) & 0xF
        words = (c[..., 0::2] | (c[..., 1::2] << 4)).reshape(k // 512, 128, 2 * n)
    return np.ascontiguousarray(words), np.ascontiguousarray(byte.astype(np.uint8).reshape(k // 512, 16, n))


def unpack_weight(words, scales, fmt):
    g, _, n = scales.shape
    words = np.ascontiguousarray(words).reshape(g, 128, n, -1)
    if fmt == "e4m3":
        vals = words.view(ml_dtypes.float8_e4m3fn).astype(np.float64)
    else:
        nib = np.empty((g, 128, n, 4), np.uint8)
        nib[..., 0::2] = words & 0xF
        nib[..., 1::2] = words >> 4
        vals = E2M1[nib]
    vals = vals * np.repeat(np.exp2(scales.astype(np.float64) - 127.0), 8, axis=1)[..., None]
    return vals.transpose(0, 1, 3, 2).reshape(g * 512, n)


def bf(x):
    return np.asarray(x, np.float32).astype(ml_dtypes.bfloat16)


def planes(Y):
    r, m = Y.shape
    b = f64(bf(Y)).reshape(r // 32, 32, m)
    amax = np.abs(b).max(1)
    byte = np.clip(np.where(amax > 0, np.frexp(amax)[1] - 1 + 127 - 7, 1), 1, 254)
    codes = (b * np.exp2(127.0 - byte)[:, None, :]).reshape(r, m).astype(np.float32).astype(ml_dtypes.float8_e4m3fn).view(np.uint8)
    words = codes.reshape(r // 512, 128, 4, m).transpose(0, 1, 3, 2)
    return np.ascontiguousarray(words), np.ascontiguousarray(byte.astype(np.uint8).reshape(r // 512, 16, m))


D, E, T, I, Q = 512, 512, 1024, 256, 512


def setup_inputs():
    n = np.random.standard_normal
    idx = np.random.permutation(T)[:I]
    fd = mx_kscale(D)
    fq = mx_kscale(Q)
    keysp = pack_weight(n((D, T)) / fd[:, None], "e4m3")
    return {
        "query": (n((D, Q)) * 0.5 / np.sqrt(D) * fd[:, None]).astype(np.float32),
        "qs": (np.random.uniform(8.0, 32.0, (Q, 1)) * fq[:, None]).astype(np.float32),
        "grows": (n((Q, E)) / fq[:, None]).astype(np.float32),
        "vals": (n((E, T))).astype(np.float32),
        "keys_words": keysp[0],
        "keys_scales": keysp[1],
        "softn": (np.random.uniform(0.3, 1.5, (E, 1))).astype(np.float32),
        "pre": (np.random.uniform(0.6, 1.6, (1, I))).astype(np.float32),
        "sg": (np.random.uniform(0.5, 2.0, (1, I))).astype(np.float32),
        "old": (0.5 * n((E, I))).astype(np.float32),
        "offs": striped(idx),
    }


def reference(query, qs, grows, vals, keys_words, keys_scales, softn, pre, sg, old, offs):
    idx = unstriped(offs)
    keysu = unpack_weight(keys_words, keys_scales, "e4m3")
    queryq = mxq(f64(query), 0, "e4m3")
    keysidxg = keysu[:, idx]
    a = queryq.T @ keysidxg
    p = np.exp(a - np.max(a, axis=1, keepdims=True))
    w = p * f64(qs) / np.sum(p, axis=1, keepdims=True)
    growsq = mxq(f64(grows), 0, "e4m3")
    wq = mxq(w, 0, "e4m3")
    c0 = growsq.T @ wq
    x1 = f64(vals)[:, idx] * f64(pre)
    dx1 = c0 / (np.square(x1) * f64(softn) + 1.0) + c0 * x1 / np.square(np.square(x1) * f64(softn) + 1.0) * (-1.0) * f64(softn) * x1 * 2.0
    y = dx1 * f64(sg) + f64(old)
    words, scales = planes(y)
    return y, words, scales

@@ -1,0 +1,250 @@
+from contextlib import ExitStack
+
+import concourse.mybir as mybir
+from concourse.masks import make_identity
+
+D, E, T, I, Q = 512, 512, 1024, 256, 512
+FLOPS = 2 * D * Q * I + 2 * Q * E * I
+
+F32 = mybir.dt.float32
+BF16 = mybir.dt.bfloat16
+I32 = mybir.dt.int32
+U32 = mybir.dt.uint32
+U16 = mybir.dt.uint16
+U8 = mybir.dt.uint8
+FP8X4 = mybir.dt.float8_e4m3fn_x4
+ALU = mybir.AluOpType
+ACT = mybir.ActivationFunctionType
+AXIS = mybir.AxisListType
+
+P = 128
+PACK = 4
+HALVES = I // P
+GROUPS = ((0, 2), (2, 3), (3, 4))
+Q_SPLIT = 88
+G_SPLIT = 88
+TINY = 2.0 ** -100
+
+
+def deal(engine_copy, grouped, raw, lo, hi):
+    engine_copy(
+        out=grouped[:, :, lo:hi, :].rearrange("p r s j -> p s j r"),
+        in_=raw[:].rearrange("p j (s r) -> p s j r", r=PACK)[:, lo:hi, :, :],
+    )
+
+
+def tile_attend_bvsoftened_d_pl_kernel(
+    tc, query, qs, grows, vals, keys_words, keys_scales, softn, pre, sg, old, offs, out_0, out_1, out_2
+):
+    nc = tc.nc
+    with ExitStack() as ctx:
+        sb = ctx.enter_context(tc.tile_pool(name="sb", bufs=1))
+        ps = ctx.enter_context(tc.psum_pool(name="ps", bufs=1))
+
+        key_bytes = sb.tile([P, T], U8, name="key_bytes", align_bytes=64)
+        nc.vector.memset(key_bytes[:].bitcast(I32), 0)
+
+        q_raw = sb.tile([P, PACK, Q], F32, name="q_raw")
+        nc.sync.dma_start(q_raw[:], query.rearrange("(p j) q -> p j q", j=PACK))
+        offsets = sb.tile([P, I // 16], U16, name="offsets")
+        nc.sync.dma_start(offsets[:], offs)
+        for quad in range(4):
+            nc.sync.dma_start(
+                key_bytes[32 * quad : 32 * quad + 4, :].bitcast(I32),
+                keys_scales[0, 4 * quad : 4 * quad + 4, :].bitcast(I32),
+            )
+        key_words = sb.tile([P, T], U32, name="key_words", align_bytes=64)
+        nc.sync.dma_start(key_words[:].bitcast(I32), keys_words[0].rearrange("p n t -> p (n t)").bitcast(I32))
+        g_raw = sb.tile([P, PACK, E], F32, name="g_raw")
+        nc.sync.dma_start(g_raw[:], grows.rearrange("(p j) e -> p j e", j=PACK))
+
+        qs_col = sb.tile([P, PACK], F32, name="qs_col")
+        nc.sync.dma_start(qs_col[:], qs.rearrange("(p r) o -> p (r o)", r=PACK))
+        soft_col = sb.tile([P, PACK], F32, name="soft_col")
+        nc.sync.dma_start(soft_col[:], softn.rearrange("(p t) o -> p (t o)", t=PACK))
+        pre_col = sb.tile([P, HALVES], F32, name="pre_col")
+        sg_col = sb.tile([P, HALVES], F32, name="sg_col")
+        with nc.allow_non_contiguous_dma(reason="one value a partition"):
+            nc.sync.dma_start(pre_col[:], pre.rearrange("o (h p) -> p (o h)", p=P))
+            nc.sync.dma_start(sg_col[:], sg.rearrange("o (h p) -> p (o h)", p=P))
+
+        vals_rows = vals.rearrange("(p t) n -> p t n", t=PACK)
+        pools = []
+        for t in range(PACK):
+            pool_t = sb.tile([P, T], F32, name=f"pool{t}")
+            nc.sync.dma_start(pool_t[:], vals_rows[:, t, :])
+            pools.append(pool_t)
+        old_rows = old.rearrange("(p t) i -> p t i", t=PACK)
+        olds = []
+        for lo, hi in GROUPS:
+            old_g = sb.tile([P, hi - lo, I], F32, name=f"old{lo}")
+            nc.sync.dma_start(old_g[:], old_rows[:, lo:hi, :])
+            olds.append(old_g)
+
+        ident = sb.tile([P, P], F32, name="ident")
+        make_identity(nc, ident[:])
+
+        k_scales = sb.tile([P, I], U8, name="k_scales", align_bytes=64)
+        nc.vector.tensor_copy(k_scales[:], key_bytes[:].indirect(offsets[:]))
+
+        q_bf = sb.tile([P, PACK, P, PACK], BF16, name="q_bf", align_bytes=64)
+        deal(nc.vector.tensor_copy, q_bf, q_raw, 0, Q_SPLIT)
+        deal(nc.scalar.copy, q_bf, q_raw, Q_SPLIT, P)
+        q_codes = sb.tile([P, Q], U32, name="q_codes", align_bytes=64)
+        q_scales = sb.tile([P, Q], U8, name="q_scales", align_bytes=64)
+        nc.vector.quantize_mx(q_codes[:].bitcast(FP8X4), q_scales[:], q_bf[:].rearrange("p r s j -> p (r s j)"))
+
+        k_codes = sb.tile([P, I], U32, name="k_codes", align_bytes=64)
+        nc.vector.tensor_copy(k_codes[:], key_words[:].indirect(offsets[:]))
+
+        neg_max = sb.tile([P, PACK], F32, name="neg_max", tag="after_exp")
+        row_sum = sb.tile([P, PACK], F32, name="row_sum")
+        p_exp = sb.tile([P, PACK, I], F32, name="p_exp")
+        for r in range(PACK):
+            score = ps.tile([P, I], F32, name=f"score{r}", tag=f"bank{r}")
+            cols = slice(r * P, (r + 1) * P)
+            nc.tensor.matmul_mx(
+                out=score[:], lhsT=q_codes[:, cols].bitcast(FP8X4), lhsT_scale=q_scales[:, cols],
+                rhs=k_codes[:].bitcast(FP8X4), rhs_scale=k_scales[:], start=True, stop=True,
+            )
+            nc.vector.tensor_reduce(neg_max[:, r : r + 1], score[:], AXIS.X, ALU.max, negate=True)
+            nc.scalar.activation(
+                p_exp[:, r, :], score[:], ACT.Exp, bias=neg_max[:, r : r + 1], accum_out=row_sum[:, r : r + 1]
+            )
+
+        g_bf = sb.tile([P, PACK, P, PACK], BF16, name="g_bf", align_bytes=64)
+        deal(nc.vector.tensor_copy, g_bf, g_raw, 0, G_SPLIT)
+        deal(nc.scalar.copy, g_bf, g_raw, G_SPLIT, P)
+
+        inv_sum = sb.tile([P, PACK], F32, name="inv_sum")
+        nc.vector.reciprocal(inv_sum[:], row_sum[:])
+
+        guess = sb.tile([P, PACK], F32, name="guess", tag="after_exp")
+        nc.scalar.activation(guess[:], soft_col[:], ACT.Abs_reciprocal_sqrt, bias=TINY)
+        root_guess = sb.tile([P, PACK], F32, name="root_guess")
+        nc.gpsimd.tensor_tensor(root_guess[:], guess[:], soft_col[:], ALU.mult)
+        near_one = sb.tile([P, PACK], F32, name="near_one")
+        nc.gpsimd.tensor_tensor(near_one[:], root_guess[:], guess[:], ALU.mult)
+        polish = sb.tile([P, PACK], F32, name="polish")
+        nc.gpsimd.tensor_scalar(polish[:], near_one[:], -0.5, 1.5, ALU.mult, ALU.add)
+        root_soft = sb.tile([P, PACK], F32, name="root_soft")
+        nc.gpsimd.tensor_tensor(root_soft[:], root_guess[:], polish[:], ALU.mult)
+        pre_sq = sb.tile([P, HALVES], F32, name="pre_sq")
+        nc.gpsimd.tensor_tensor(pre_sq[:], pre_col[:], pre_col[:], ALU.mult)
+        sg_two = sb.tile([P, HALVES], F32, name="sg_two")
+        nc.gpsimd.tensor_tensor(sg_two[:], sg_col[:], sg_col[:], ALU.add)
+
+        u_banks = {}
+
+        def look_up(t):
+            g = [lo <= t < hi for lo, hi in GROUPS].index(True)
+            lo, hi = GROUPS[g]
+            if t == lo:
+                u_banks[g] = ps.tile([P, HALVES, hi - lo, P], F32, name=f"u_t{g}", tag=f"bank{g}")
+            picked = sb.tile([P, I], F32, name=f"picked{t}")
+            nc.vector.tensor_copy(picked[:], pools[t][:].indirect(offsets[:]))
+            soft_sq = sb.tile([P, I], F32, name=f"soft_sq{t}")
+            nc.scalar.activation(soft_sq[:], picked[:], ACT.Square, scale=root_soft[:, t : t + 1])
+            for h in range(HALVES):
+                nc.tensor.transpose(u_banks[g][:, h, t - lo, :], soft_sq[:, h * P : (h + 1) * P], ident[:])
+
+        recips = {}
+
+        def invert(g):
+            n = GROUPS[g][1] - GROUPS[g][0]
+            s_sq = sb.tile([P, HALVES, n * P], F32, name=f"s_sq{g}")
+            for h in range(HALVES):
+                nc.scalar.activation(
+                    s_sq[:, h, :], u_banks[g][:, h, :, :].rearrange("p t e -> p (t e)"), ACT.Square,
+                    scale=pre_sq[:, h : h + 1], bias=1.0,
+                )
+            recips[g] = sb.tile([P, HALVES * n * P], F32, name=f"recip{g}")
+            nc.scalar.activation(recips[g][:], s_sq[:].rearrange("p h e -> p (h e)"), ACT.Abs_reciprocal_sqrt)
+
+        look_up(0)
+        row_factor = sb.tile([P, PACK], F32, name="row_factor")
+        nc.vector.tensor_tensor(row_factor[:], inv_sum[:], qs_col[:], ALU.mult)
+        g_codes = sb.tile([P, E], U32, name="g_codes", align_bytes=64)
+        g_scales = sb.tile([P, E], U8, name="g_scales", align_bytes=64)
+        nc.vector.quantize_mx(g_codes[:].bitcast(FP8X4), g_scales[:], g_bf[:].rearrange("p r s j -> p (r s j)"))
+
+        w_bf = sb.tile([P, I, PACK], BF16, name="w_bf", align_bytes=64)
+        w_codes = sb.tile([P, I], U32, name="w_codes", align_bytes=64)
+        w_scales = sb.tile([P, I], U8, name="w_scales", align_bytes=64)
+        runs = I // PACK
+        nc.vector.tensor_tensor(
+            w_bf[:].rearrange("p (c i) r -> p c r i", i=PACK),
+            p_exp[:].rearrange("p r (c i) -> p c r i", i=PACK),
+            row_factor[:].unsqueeze(1).unsqueeze(3).to_broadcast([P, runs, PACK, PACK]),
+            ALU.mult,
+        )
+        look_up(1)
+        nc.vector.quantize_mx(w_codes[:].bitcast(FP8X4), w_scales[:], w_bf[:].rearrange("p i r -> p (i r)"))
+
+        c0 = []
+        for h in range(HALVES):
+            c0_h = ps.tile([P, E], F32, name=f"c0_{h}")
+            cols = slice(h * P, (h + 1) * P)
+            nc.tensor.matmul_mx(
+                out=c0_h[:], lhsT=w_codes[:, cols].bitcast(FP8X4), lhsT_scale=w_scales[:, cols],
+                rhs=g_codes[:].bitcast(FP8X4), rhs_scale=g_scales[:], start=True, stop=True,
+            )
+            c0.append(c0_h)
+
+        invert(0)
+        look_up(2)
+        look_up(3)
+        invert(1)
+        invert(2)
+
+        y = sb.tile([P, PACK, I], F32, name="y")
+        y_rows = out_0.rearrange("(p t) i -> p t i", t=PACK)
+        y_bf = sb.tile([P, I, PACK], BF16, name="y_bf", align_bytes=64)
+        backs = {}
+
+        def chain(g):
+            lo, hi = GROUPS[g]
+            n = hi - lo
+            slope = sb.tile([P, HALVES, n * P], F32, name=f"slope{g}")
+            nc.vector.scalar_tensor_tensor(
+                slope[:].rearrange("p h e -> p (h e)"), recips[g][:], 0.5, recips[g][:], ALU.subtract, ALU.mult
+            )
+            dx = sb.tile([P, HALVES, n * P], F32, name=f"dx{g}")
+            for h in range(HALVES):
+                nc.vector.scalar_tensor_tensor(
+                    dx[:, h, :], c0[h][:, lo * P : hi * P], sg_two[:, h : h + 1], slope[:, h, :], ALU.mult, ALU.mult
+                )
+            backs[g] = ps.tile([P, n, I], F32, name=f"back{g}", tag=f"bank{g}")
+            for t in range(n):
+                for h in range(HALVES):
+                    nc.tensor.transpose(backs[g][:, t, h * P : (h + 1) * P], dx[:, h, t * P : (t + 1) * P], ident[:])
+
+        def finish(g):
+            lo, hi = GROUPS[g]
+            nc.vector.tensor_tensor(y[:, lo:hi, :], backs[g][:], olds[g][:], ALU.add)
+            nc.sync.dma_start(y_rows[:, lo:hi, :], y[:, lo:hi, :])
+
+        def round_pair(copy, lo):
+            copy(
+                out=y_bf[:, :, lo : lo + 2].rearrange("p (c i) t -> p c t i", i=PACK),
+                in_=y[:, lo : lo + 2, :].rearrange("p t (c i) -> p c t i", i=PACK),
+            )
+
+        chain(0)
+        chain(1)
+        finish(0)
+        round_pair(nc.scalar.copy, 0)
+        chain(2)
+        finish(1)
+        finish(2)
+        round_pair(nc.vector.tensor_copy, 2)
+        y_codes = sb.tile([P, I], U32, name="y_codes", align_bytes=64)
+        y_scales = sb.tile([P, I], U8, name="y_scales", align_bytes=64)
+        nc.vector.quantize_mx(y_codes[:].bitcast(FP8X4), y_scales[:], y_bf[:].rearrange("p i t -> p (i t)"))
+        nc.sync.dma_start(out_1[0].rearrange("p c r -> p (c r)").bitcast(I32), y_codes[:].bitcast(I32))
+        for quad in range(4):
+            queue = nc.scalar if quad % 2 == 0 else nc.sync
+            queue.dma_start(
+                out_2[0, 4 * quad : 4 * quad + 4, :].bitcast(I32),
+                y_scales[32 * quad : 32 * quad + 4, :].bitcast(I32),
+            )

@@ -20,16 +20,17 @@ AXIS = mybir.AxisListType
 P = 128
 PACK = 4
 HALVES = I // P
-GROUPS = ((0, 2), (2, 3), (3, 4))
-Q_SPLIT = 88
+GROUPS = ((0, 1), (1, 3), (3, 4))
+Y_SPLIT = 176
+BANKS = ("spare", "bank0", "bank1")
+PICK_AFTER = ("key_words", "max1", "max3", "pool2")
 G_SPLIT = 88
-TINY = 2.0 ** -100
 
 
 def deal(engine_copy, grouped, raw, lo, hi):
     engine_copy(
         out=grouped[:, :, lo:hi, :].rearrange("p r s j -> p s j r"),
-        in_=raw[:].rearrange("p j (s r) -> p s j r", r=PACK)[:, lo:hi, :, :],
+        in_=raw.rearrange("p j (s r) -> p s j r", r=PACK)[:, lo:hi, :, :],
     )
 
 
@@ -44,8 +45,11 @@ def tile_attend_bvsoftened_d_pl_kernel(
         key_bytes = sb.tile([P, T], U8, name="key_bytes", align_bytes=64)
         nc.vector.memset(key_bytes[:].bitcast(I32), 0)
 
-        q_raw = sb.tile([P, PACK, Q], F32, name="q_raw")
-        nc.sync.dma_start(q_raw[:], query.rearrange("(p j) q -> p j q", j=PACK))
+        ident = sb.tile([P, P], F32, name="ident")
+        make_identity(nc, ident[:])
+        q_rows = query.rearrange("(p j) q -> p j q", j=PACK)
+        q_raw0 = sb.tile([P, PACK, Q // 2], F32, name="q_raw0")
+        nc.sync.dma_start(q_raw0[:], q_rows[:, :, 0 : Q // 2])
         offsets = sb.tile([P, I // 16], U16, name="offsets")
         nc.sync.dma_start(offsets[:], offs)
         for quad in range(4):
@@ -53,27 +57,33 @@ def tile_attend_bvsoftened_d_pl_kernel(
                 key_bytes[32 * quad : 32 * quad + 4, :].bitcast(I32),
                 keys_scales[0, 4 * quad : 4 * quad + 4, :].bitcast(I32),
             )
-        key_words = sb.tile([P, T], U32, name="key_words", align_bytes=64)
+        q_raw1 = sb.tile([P, PACK, Q // 2], F32, name="q_raw1", tag="q_raw1", align_bytes=64)
+        nc.sync.dma_start(q_raw1[:], q_rows[:, :, Q // 2 : Q])
+        key_words = sb.tile([P, T], U32, name="key_words", tag="key_words", align_bytes=64)
         nc.sync.dma_start(key_words[:].bitcast(I32), keys_words[0].rearrange("p n t -> p (n t)").bitcast(I32))
-        g_raw = sb.tile([P, PACK, E], F32, name="g_raw")
-        nc.sync.dma_start(g_raw[:], grows.rearrange("(p j) e -> p j e", j=PACK))
 
-        qs_col = sb.tile([P, PACK], F32, name="qs_col")
-        nc.sync.dma_start(qs_col[:], qs.rearrange("(p r) o -> p (r o)", r=PACK))
         soft_col = sb.tile([P, PACK], F32, name="soft_col")
         nc.sync.dma_start(soft_col[:], softn.rearrange("(p t) o -> p (t o)", t=PACK))
-        pre_col = sb.tile([P, HALVES], F32, name="pre_col")
-        sg_col = sb.tile([P, HALVES], F32, name="sg_col")
-        with nc.allow_non_contiguous_dma(reason="one value a partition"):
-            nc.sync.dma_start(pre_col[:], pre.rearrange("o (h p) -> p (o h)", p=P))
-            nc.sync.dma_start(sg_col[:], sg.rearrange("o (h p) -> p (o h)", p=P))
-
         vals_rows = vals.rearrange("(p t) n -> p t n", t=PACK)
         pools = []
         for t in range(PACK):
-            pool_t = sb.tile([P, T], F32, name=f"pool{t}")
+            pool_t = sb.tile([P, T], F32, name=f"pool{t}", tag=f"pool{t}", align_bytes=64)
             nc.sync.dma_start(pool_t[:], vals_rows[:, t, :])
             pools.append(pool_t)
+            if t == 0:
+                qs_col = sb.tile([P, PACK], F32, name="qs_col")
+                nc.sync.dma_start(qs_col[:], qs.rearrange("(p r) o -> p (r o)", r=PACK))
+                pre_col = sb.tile([P, HALVES], F32, name="pre_col")
+                sg_col = sb.tile([P, HALVES], F32, name="sg_col")
+                with nc.allow_non_contiguous_dma(reason="one value a partition"):
+                    nc.sync.dma_start(pre_col[:], pre.rearrange("o (h p) -> p (o h)", p=P))
+                    nc.sync.dma_start(sg_col[:], sg.rearrange("o (h p) -> p (o h)", p=P))
+        g_rows = grows.rearrange("(p j) e -> p j e", j=PACK)
+        g_raw = []
+        for half in range(2):
+            g_half = sb.tile([P, PACK, E // 2], F32, name=f"g_raw{half}")
+            nc.sync.dma_start(g_half[:], g_rows[:, :, half * E // 2 : (half + 1) * E // 2])
+            g_raw.append(g_half)
         old_rows = old.rearrange("(p t) i -> p t i", t=PACK)
         olds = []
         for lo, hi in GROUPS:
@@ -81,25 +91,87 @@ def tile_attend_bvsoftened_d_pl_kernel(
             nc.sync.dma_start(old_g[:], old_rows[:, lo:hi, :])
             olds.append(old_g)
 
-        ident = sb.tile([P, P], F32, name="ident")
-        make_identity(nc, ident[:])
-
-        k_scales = sb.tile([P, I], U8, name="k_scales", align_bytes=64)
-        nc.vector.tensor_copy(k_scales[:], key_bytes[:].indirect(offsets[:]))
+        root_soft = sb.tile([P, PACK], F32, name="root_soft")
+        half = sb.tile([P, PACK], F32, name="half")
+        nc.gpsimd.memset(half[:], 0.5)
+        nc.gpsimd.tensor_tensor(root_soft[:], soft_col[:], half[:], ALU.pow)
 
         q_bf = sb.tile([P, PACK, P, PACK], BF16, name="q_bf", align_bytes=64)
-        deal(nc.vector.tensor_copy, q_bf, q_raw, 0, Q_SPLIT)
-        deal(nc.scalar.copy, q_bf, q_raw, Q_SPLIT, P)
+        deal(nc.vector.tensor_copy, q_bf[:, :, 0 : P // 2, :], q_raw0[:], 0, P // 2)
+        k_scales = sb.tile([P, I], U8, name="k_scales", align_bytes=64)
+        nc.vector.tensor_copy(k_scales[:], key_bytes[:].indirect(offsets[:]))
+        deal(nc.vector.tensor_copy, q_bf[:, :, P // 2 : P, :], q_raw1[:], 0, P // 2)
         q_codes = sb.tile([P, Q], U32, name="q_codes", align_bytes=64)
         q_scales = sb.tile([P, Q], U8, name="q_scales", align_bytes=64)
-        nc.vector.quantize_mx(q_codes[:].bitcast(FP8X4), q_scales[:], q_bf[:].rearrange("p r s j -> p (r s j)"))
 
-        k_codes = sb.tile([P, I], U32, name="k_codes", align_bytes=64)
+        def quantise_queries(lo, hi):
+            cols = slice(lo * P, hi * P)
+            nc.vector.quantize_mx(
+                q_codes[:, cols].bitcast(FP8X4), q_scales[:, cols], q_bf[:, lo:hi].rearrange("p r s j -> p (r s j)")
+            )
+
+        quantise_queries(0, 2)
+        k_codes = sb.tile([P, I], U32, name="k_codes", tag="q_raw1", align_bytes=64)
         nc.vector.tensor_copy(k_codes[:], key_words[:].indirect(offsets[:]))
+        quantise_queries(2, 4)
 
-        neg_max = sb.tile([P, PACK], F32, name="neg_max", tag="after_exp")
+        picks = {}
+
+        def pick(t):
+            picks[t] = sb.tile([P, I], F32, name=f"picked{t}", tag=PICK_AFTER[t], align_bytes=64)
+            nc.vector.tensor_copy(picks[t][:], pools[t][:].indirect(offsets[:]))
+
+        u_banks = {}
+        squares = {}
+
+        def look_up(t):
+            g = [lo <= t < hi for lo, hi in GROUPS].index(True)
+            lo, hi = GROUPS[g]
+            if t == lo:
+                u_banks[g] = ps.tile([P, HALVES, hi - lo, P], F32, name=f"u_t{g}", tag=BANKS[g])
+            if t < 2:
+                squares[t] = sb.tile([P, 1, I], F32, name=f"soft_sq{t}", tag=f"soft_sq{t}", align_bytes=64)
+            elif t == 2:
+                squares[t] = sb.tile([P, 2, I], F32, name="soft_sq2", tag="soft_sq1", align_bytes=64)
+            soft_sq = squares[min(t, 2)][:, max(t - 2, 0), :]
+            nc.scalar.activation(soft_sq, picks[t][:], ACT.Square, scale=root_soft[:, t : t + 1])
+            for h in range(HALVES):
+                nc.tensor.transpose(u_banks[g][:, h, t - lo, :], soft_sq[:, h * P : (h + 1) * P], ident[:])
+
+        recips = {}
+
+        s_squares = {}
+
+        def square_up(g):
+            n = GROUPS[g][1] - GROUPS[g][0]
+            s_sq = sb.tile([P, HALVES, n * P], F32, name=f"s_sq{g}", tag="max2" if g == 0 else f"s_sq{g}", align_bytes=64)
+            s_squares[g] = s_sq
+            for h in range(HALVES):
+                nc.scalar.activation(
+                    s_sq[:, h, :], u_banks[g][:, h, :, :].rearrange("p t e -> p (t e)"), ACT.Square,
+                    scale=pre_sq[:, h : h + 1], bias=1.0,
+                )
+
+        def invert(g):
+            n = GROUPS[g][1] - GROUPS[g][0]
+            s_sq = s_squares[g]
+            recips[g] = sb.tile([P, HALVES * n * P], F32, name=f"recip{g}", tag="max1" if g == 0 else f"recip{g}", align_bytes=64)
+            nc.scalar.activation(recips[g][:], s_sq[:].rearrange("p h e -> p (h e)"), ACT.Abs_reciprocal_sqrt)
+
+        slopes = {}
+
+        def slope_of(g):
+            n = GROUPS[g][1] - GROUPS[g][0]
+            lo = GROUPS[g][0]
+            slopes[g] = all_slopes[:, lo * I : (lo + n) * I].rearrange("p (h e) -> p h e", h=HALVES)
+            nc.vector.scalar_tensor_tensor(
+                all_slopes[:, lo * I : (lo + n) * I], recips[g][:], 0.5, recips[g][:], ALU.subtract, ALU.mult
+            )
+
+        pick(0)
+        look_up(0)
         row_sum = sb.tile([P, PACK], F32, name="row_sum")
-        p_exp = sb.tile([P, PACK, I], F32, name="p_exp")
+        p_exp = sb.tile([P, PACK, I], F32, name="p_exp", tag="p_exp", align_bytes=64)
         for r in range(PACK):
             score = ps.tile([P, I], F32, name=f"score{r}", tag=f"bank{r}")
             cols = slice(r * P, (r + 1) * P)
@@ -107,70 +179,28 @@ def tile_attend_bvsoftened_d_pl_kernel(
                 out=score[:], lhsT=q_codes[:, cols].bitcast(FP8X4), lhsT_scale=q_scales[:, cols],
                 rhs=k_codes[:].bitcast(FP8X4), rhs_scale=k_scales[:], start=True, stop=True,
             )
-            nc.vector.tensor_reduce(neg_max[:, r : r + 1], score[:], AXIS.X, ALU.max, negate=True)
+            neg_max = sb.tile([P, 1], F32, name=f"neg_max{r}", tag=f"max{r}", align_bytes=64)
+            nc.vector.tensor_reduce(neg_max[:], score[:], AXIS.X, ALU.max, negate=True)
             nc.scalar.activation(
-                p_exp[:, r, :], score[:], ACT.Exp, bias=neg_max[:, r : r + 1], accum_out=row_sum[:, r : r + 1]
+                p_exp[:, r, :], score[:], ACT.Exp, bias=neg_max[:], accum_out=row_sum[:, r : r + 1]
             )
 
-        g_bf = sb.tile([P, PACK, P, PACK], BF16, name="g_bf", align_bytes=64)
-        deal(nc.vector.tensor_copy, g_bf, g_raw, 0, G_SPLIT)
-        deal(nc.scalar.copy, g_bf, g_raw, G_SPLIT, P)
-
-        inv_sum = sb.tile([P, PACK], F32, name="inv_sum")
-        nc.vector.reciprocal(inv_sum[:], row_sum[:])
-
-        guess = sb.tile([P, PACK], F32, name="guess", tag="after_exp")
-        nc.scalar.activation(guess[:], soft_col[:], ACT.Abs_reciprocal_sqrt, bias=TINY)
-        root_guess = sb.tile([P, PACK], F32, name="root_guess")
-        nc.gpsimd.tensor_tensor(root_guess[:], guess[:], soft_col[:], ALU.mult)
-        near_one = sb.tile([P, PACK], F32, name="near_one")
-        nc.gpsimd.tensor_tensor(near_one[:], root_guess[:], guess[:], ALU.mult)
-        polish = sb.tile([P, PACK], F32, name="polish")
-        nc.gpsimd.tensor_scalar(polish[:], near_one[:], -0.5, 1.5, ALU.mult, ALU.add)
-        root_soft = sb.tile([P, PACK], F32, name="root_soft")
-        nc.gpsimd.tensor_tensor(root_soft[:], root_guess[:], polish[:], ALU.mult)
         pre_sq = sb.tile([P, HALVES], F32, name="pre_sq")
-        nc.gpsimd.tensor_tensor(pre_sq[:], pre_col[:], pre_col[:], ALU.mult)
+        nc.scalar.activation(pre_sq[:], pre_col[:], ACT.Square)
         sg_two = sb.tile([P, HALVES], F32, name="sg_two")
-        nc.gpsimd.tensor_tensor(sg_two[:], sg_col[:], sg_col[:], ALU.add)
+        nc.scalar.activation(sg_two[:], sg_col[:], ACT.Copy, scale=2.0)
 
-        u_banks = {}
-
-        def look_up(t):
-            g = [lo <= t < hi for lo, hi in GROUPS].index(True)
-            lo, hi = GROUPS[g]
-            if t == lo:
-                u_banks[g] = ps.tile([P, HALVES, hi - lo, P], F32, name=f"u_t{g}", tag=f"bank{g}")
-            picked = sb.tile([P, I], F32, name=f"picked{t}")
-            nc.vector.tensor_copy(picked[:], pools[t][:].indirect(offsets[:]))
-            soft_sq = sb.tile([P, I], F32, name=f"soft_sq{t}")
-            nc.scalar.activation(soft_sq[:], picked[:], ACT.Square, scale=root_soft[:, t : t + 1])
-            for h in range(HALVES):
-                nc.tensor.transpose(u_banks[g][:, h, t - lo, :], soft_sq[:, h * P : (h + 1) * P], ident[:])
-
-        recips = {}
-
-        def invert(g):
-            n = GROUPS[g][1] - GROUPS[g][0]
-            s_sq = sb.tile([P, HALVES, n * P], F32, name=f"s_sq{g}")
-            for h in range(HALVES):
-                nc.scalar.activation(
-                    s_sq[:, h, :], u_banks[g][:, h, :, :].rearrange("p t e -> p (t e)"), ACT.Square,
-                    scale=pre_sq[:, h : h + 1], bias=1.0,
-                )
-            recips[g] = sb.tile([P, HALVES * n * P], F32, name=f"recip{g}")
-            nc.scalar.activation(recips[g][:], s_sq[:].rearrange("p h e -> p (h e)"), ACT.Abs_reciprocal_sqrt)
-
-        look_up(0)
+        square_up(0)
+        pick(1)
+        look_up(1)
+        invert(0)
+        inv_sum = sb.tile([P, PACK], F32, name="inv_sum", tag="inv_sum", align_bytes=64)
+        nc.vector.reciprocal(inv_sum[:], row_sum[:])
+        pick(2)
         row_factor = sb.tile([P, PACK], F32, name="row_factor")
         nc.vector.tensor_tensor(row_factor[:], inv_sum[:], qs_col[:], ALU.mult)
-        g_codes = sb.tile([P, E], U32, name="g_codes", align_bytes=64)
-        g_scales = sb.tile([P, E], U8, name="g_scales", align_bytes=64)
-        nc.vector.quantize_mx(g_codes[:].bitcast(FP8X4), g_scales[:], g_bf[:].rearrange("p r s j -> p (r s j)"))
-
+        pick(3)
         w_bf = sb.tile([P, I, PACK], BF16, name="w_bf", align_bytes=64)
-        w_codes = sb.tile([P, I], U32, name="w_codes", align_bytes=64)
-        w_scales = sb.tile([P, I], U8, name="w_scales", align_bytes=64)
         runs = I // PACK
         nc.vector.tensor_tensor(
             w_bf[:].rearrange("p (c i) r -> p c r i", i=PACK),
@@ -178,24 +208,40 @@ def tile_attend_bvsoftened_d_pl_kernel(
             row_factor[:].unsqueeze(1).unsqueeze(3).to_broadcast([P, runs, PACK, PACK]),
             ALU.mult,
         )
-        look_up(1)
+        g_bf = sb.tile([P, PACK, P, PACK], BF16, name="g_bf", tag="pool3", align_bytes=64)
+        deal(nc.vector.tensor_copy, g_bf[:, :, 0 : P // 2, :], g_raw[0][:], 0, P // 2)
+        w_codes = sb.tile([P, I], U32, name="w_codes", align_bytes=64)
+        w_scales = sb.tile([P, I], U8, name="w_scales", align_bytes=64)
         nc.vector.quantize_mx(w_codes[:].bitcast(FP8X4), w_scales[:], w_bf[:].rearrange("p i r -> p (i r)"))
-
-        c0 = []
-        for h in range(HALVES):
-            c0_h = ps.tile([P, E], F32, name=f"c0_{h}")
-            cols = slice(h * P, (h + 1) * P)
-            nc.tensor.matmul_mx(
-                out=c0_h[:], lhsT=w_codes[:, cols].bitcast(FP8X4), lhsT_scale=w_scales[:, cols],
-                rhs=g_codes[:].bitcast(FP8X4), rhs_scale=g_scales[:], start=True, stop=True,
-            )
-            c0.append(c0_h)
-
-        invert(0)
+        deal(nc.vector.tensor_copy, g_bf[:, :, P // 2 : P, :], g_raw[1][:], 0, P // 2)
         look_up(2)
         look_up(3)
+
+        g_codes = sb.tile([P, E], U32, name="g_codes", tag=PICK_AFTER[3], align_bytes=64)
+        g_scales = sb.tile([P, E], U8, name="g_scales", align_bytes=64)
+        for pair in range(2):
+            feats = slice(2 * pair * P, 2 * (pair + 1) * P)
+            nc.vector.quantize_mx(
+                g_codes[:, feats].bitcast(FP8X4), g_scales[:, feats],
+                g_bf[:, 2 * pair : 2 * pair + 2].rearrange("p r s j -> p (r s j)"),
+            )
+        all_slopes = sb.tile([P, PACK * I], F32, name="all_slopes", tag="pool3", align_bytes=64)
+        slope_of(0)
+        square_up(1)
+        square_up(2)
         invert(1)
         invert(2)
+
+        c0 = {}
+        for g, (lo, hi) in enumerate(GROUPS):
+            c0[g] = ps.tile([P, HALVES, (hi - lo) * P], F32, name=f"c0_{g}")
+            feats = slice(lo * P, hi * P)
+            for h in range(HALVES):
+                cols = slice(h * P, (h + 1) * P)
+                nc.tensor.matmul_mx(
+                    out=c0[g][:, h, :], lhsT=w_codes[:, cols].bitcast(FP8X4), lhsT_scale=w_scales[:, cols],
+                    rhs=g_codes[:, feats].bitcast(FP8X4), rhs_scale=g_scales[:, feats], start=True, stop=True,
+                )
 
         y = sb.tile([P, PACK, I], F32, name="y")
         y_rows = out_0.rearrange("(p t) i -> p t i", t=PACK)
@@ -205,16 +251,13 @@ def tile_attend_bvsoftened_d_pl_kernel(
         def chain(g):
             lo, hi = GROUPS[g]
             n = hi - lo
-            slope = sb.tile([P, HALVES, n * P], F32, name=f"slope{g}")
-            nc.vector.scalar_tensor_tensor(
-                slope[:].rearrange("p h e -> p (h e)"), recips[g][:], 0.5, recips[g][:], ALU.subtract, ALU.mult
-            )
+            slope = slopes[g]
             dx = sb.tile([P, HALVES, n * P], F32, name=f"dx{g}")
             for h in range(HALVES):
                 nc.vector.scalar_tensor_tensor(
-                    dx[:, h, :], c0[h][:, lo * P : hi * P], sg_two[:, h : h + 1], slope[:, h, :], ALU.mult, ALU.mult
+                    dx[:, h, :], c0[g][:, h, :], sg_two[:, h : h + 1], slope[:, h, :], ALU.mult, ALU.mult
                 )
-            backs[g] = ps.tile([P, n, I], F32, name=f"back{g}", tag=f"bank{g}")
+            backs[g] = ps.tile([P, n, I], F32, name=f"back{g}", tag=BANKS[g])
             for t in range(n):
                 for h in range(HALVES):
                     nc.tensor.transpose(backs[g][:, t, h * P : (h + 1) * P], dx[:, h, t * P : (t + 1) * P], ident[:])
@@ -224,20 +267,22 @@ def tile_attend_bvsoftened_d_pl_kernel(
             nc.vector.tensor_tensor(y[:, lo:hi, :], backs[g][:], olds[g][:], ALU.add)
             nc.sync.dma_start(y_rows[:, lo:hi, :], y[:, lo:hi, :])
 
-        def round_pair(copy, lo):
+        def round_columns(copy, lo, hi):
             copy(
-                out=y_bf[:, :, lo : lo + 2].rearrange("p (c i) t -> p c t i", i=PACK),
-                in_=y[:, lo : lo + 2, :].rearrange("p t (c i) -> p c t i", i=PACK),
+                out=y_bf[:, lo:hi, :].rearrange("p (c i) t -> p c t i", i=PACK),
+                in_=y[:, :, lo:hi].rearrange("p t (c i) -> p c t i", i=PACK),
             )
 
         chain(0)
+        slope_of(1)
+        slope_of(2)
         chain(1)
         finish(0)
-        round_pair(nc.scalar.copy, 0)
         chain(2)
         finish(1)
         finish(2)
-        round_pair(nc.vector.tensor_copy, 2)
+        round_columns(nc.vector.tensor_copy, 0, Y_SPLIT)
+        round_columns(nc.scalar.copy, Y_SPLIT, I)
         y_codes = sb.tile([P, I], U32, name="y_codes", align_bytes=64)
         y_scales = sb.tile([P, I], U8, name="y_scales", align_bytes=64)
         nc.vector.quantize_mx(y_codes[:].bitcast(FP8X4), y_scales[:], y_bf[:].rearrange("p i t -> p (i t)"))

@@ -21,10 +21,7 @@ P = 128
 PACK = 4
 HALVES = I // P
 GROUPS = ((0, 1), (1, 3), (3, 4))
-Y_SPLIT = 176
 BANKS = ("spare", "bank0", "bank1")
-PICK_AFTER = ("key_words", "max1", "max3", "pool2")
-G_SPLIT = 88
 
 
 def deal(engine_copy, grouped, raw, lo, hi):
@@ -57,7 +54,7 @@ def tile_attend_bvsoftened_d_pl_kernel(
                 key_bytes[32 * quad : 32 * quad + 4, :].bitcast(I32),
                 keys_scales[0, 4 * quad : 4 * quad + 4, :].bitcast(I32),
             )
-        q_raw1 = sb.tile([P, PACK, Q // 2], F32, name="q_raw1", tag="q_raw1", align_bytes=64)
+        q_raw1 = sb.tile([P, PACK, Q // 2], F32, name="q_raw1")
         nc.sync.dma_start(q_raw1[:], q_rows[:, :, Q // 2 : Q])
         key_words = sb.tile([P, T], U32, name="key_words", tag="key_words", align_bytes=64)
         nc.sync.dma_start(key_words[:].bitcast(I32), keys_words[0].rearrange("p n t -> p (n t)").bitcast(I32))
@@ -78,18 +75,10 @@ def tile_attend_bvsoftened_d_pl_kernel(
                 with nc.allow_non_contiguous_dma(reason="one value a partition"):
                     nc.sync.dma_start(pre_col[:], pre.rearrange("o (h p) -> p (o h)", p=P))
                     nc.sync.dma_start(sg_col[:], sg.rearrange("o (h p) -> p (o h)", p=P))
-        g_rows = grows.rearrange("(p j) e -> p j e", j=PACK)
-        g_raw = []
-        for half in range(2):
-            g_half = sb.tile([P, PACK, E // 2], F32, name=f"g_raw{half}")
-            nc.sync.dma_start(g_half[:], g_rows[:, :, half * E // 2 : (half + 1) * E // 2])
-            g_raw.append(g_half)
-        old_rows = old.rearrange("(p t) i -> p t i", t=PACK)
-        olds = []
-        for lo, hi in GROUPS:
-            old_g = sb.tile([P, hi - lo, I], F32, name=f"old{lo}")
-            nc.sync.dma_start(old_g[:], old_rows[:, lo:hi, :])
-            olds.append(old_g)
+        g_raw = sb.tile([P, PACK, E], F32, name="g_raw", tag="g_raw", align_bytes=64)
+        nc.sync.dma_start(g_raw[:], grows.rearrange("(p j) e -> p j e", j=PACK))
+        old_sb = sb.tile([P, PACK, I], F32, name="old_sb")
+        nc.sync.dma_start(old_sb[:], old.rearrange("(p t) i -> p t i", t=PACK))
 
         root_soft = sb.tile([P, PACK], F32, name="root_soft")
         half = sb.tile([P, PACK], F32, name="half")
@@ -103,38 +92,25 @@ def tile_attend_bvsoftened_d_pl_kernel(
         deal(nc.vector.tensor_copy, q_bf[:, :, P // 2 : P, :], q_raw1[:], 0, P // 2)
         q_codes = sb.tile([P, Q], U32, name="q_codes", align_bytes=64)
         q_scales = sb.tile([P, Q], U8, name="q_scales", align_bytes=64)
-
-        def quantise_queries(lo, hi):
-            cols = slice(lo * P, hi * P)
-            nc.vector.quantize_mx(
-                q_codes[:, cols].bitcast(FP8X4), q_scales[:, cols], q_bf[:, lo:hi].rearrange("p r s j -> p (r s j)")
-            )
-
-        quantise_queries(0, 2)
-        k_codes = sb.tile([P, I], U32, name="k_codes", tag="q_raw1", align_bytes=64)
+        nc.vector.quantize_mx(q_codes[:].bitcast(FP8X4), q_scales[:], q_bf[:].rearrange("p r s j -> p (r s j)"))
+        k_codes = sb.tile([P, I], U32, name="k_codes", align_bytes=64)
         nc.vector.tensor_copy(k_codes[:], key_words[:].indirect(offsets[:]))
-        quantise_queries(2, 4)
 
         picks = {}
 
         def pick(t):
-            picks[t] = sb.tile([P, I], F32, name=f"picked{t}", tag=PICK_AFTER[t], align_bytes=64)
+            picks[t] = sb.tile([P, I], F32, name=f"picked{t}", tag=f"picked{t}", align_bytes=64)
             nc.vector.tensor_copy(picks[t][:], pools[t][:].indirect(offsets[:]))
 
         u_banks = {}
-        squares = {}
 
         def look_up(t):
             g = [lo <= t < hi for lo, hi in GROUPS].index(True)
             lo, hi = GROUPS[g]
             if t == lo:
                 u_banks[g] = ps.tile([P, HALVES, hi - lo, P], F32, name=f"u_t{g}", tag=BANKS[g])
-            if t < 2:
-                squares[t] = sb.tile([P, 1, I], F32, name=f"soft_sq{t}", tag=f"soft_sq{t}", align_bytes=64)
-            elif t == 2:
-                squares[t] = sb.tile([P, 2, I], F32, name="soft_sq2", tag="soft_sq1", align_bytes=64)
-            soft_sq = squares[min(t, 2)][:, max(t - 2, 0), :]
-            nc.scalar.activation(soft_sq, picks[t][:], ACT.Square, scale=root_soft[:, t : t + 1])
+            soft_sq = sb.tile([P, I], F32, name=f"soft_sq{t}", tag=f"soft_sq{t}", align_bytes=64)
+            nc.scalar.activation(soft_sq[:], picks[t][:], ACT.Square, scale=root_soft[:, t : t + 1])
             for h in range(HALVES):
                 nc.tensor.transpose(u_banks[g][:, h, t - lo, :], soft_sq[:, h * P : (h + 1) * P], ident[:])
 
@@ -144,7 +120,7 @@ def tile_attend_bvsoftened_d_pl_kernel(
 
         def square_up(g):
             n = GROUPS[g][1] - GROUPS[g][0]
-            s_sq = sb.tile([P, HALVES, n * P], F32, name=f"s_sq{g}", tag="max2" if g == 0 else f"s_sq{g}", align_bytes=64)
+            s_sq = sb.tile([P, HALVES, n * P], F32, name=f"s_sq{g}", tag=("pool0", "picked3", "s_sq2")[g], align_bytes=64)
             s_squares[g] = s_sq
             for h in range(HALVES):
                 nc.scalar.activation(
@@ -155,23 +131,25 @@ def tile_attend_bvsoftened_d_pl_kernel(
         def invert(g):
             n = GROUPS[g][1] - GROUPS[g][0]
             s_sq = s_squares[g]
-            recips[g] = sb.tile([P, HALVES * n * P], F32, name=f"recip{g}", tag="max1" if g == 0 else f"recip{g}", align_bytes=64)
+            recips[g] = sb.tile([P, HALVES * n * P], F32, name=f"recip{g}", tag=("picked2", "soft_sq3", "recip2")[g], align_bytes=64)
             nc.scalar.activation(recips[g][:], s_sq[:].rearrange("p h e -> p (h e)"), ACT.Abs_reciprocal_sqrt)
 
         slopes = {}
 
         def slope_of(g):
             n = GROUPS[g][1] - GROUPS[g][0]
-            lo = GROUPS[g][0]
-            slopes[g] = all_slopes[:, lo * I : (lo + n) * I].rearrange("p (h e) -> p h e", h=HALVES)
+            slopes[g] = sb.tile(
+                [P, HALVES, n * P], F32, name=f"slope{g}", tag=("slope0", "picked0", "g_raw")[g], align_bytes=64
+            )
             nc.vector.scalar_tensor_tensor(
-                all_slopes[:, lo * I : (lo + n) * I], recips[g][:], 0.5, recips[g][:], ALU.subtract, ALU.mult
+                slopes[g][:].rearrange("p h e -> p (h e)"), recips[g][:], 0.5, recips[g][:], ALU.subtract, ALU.mult
             )
 
         pick(0)
         look_up(0)
+        neg_max = sb.tile([P, PACK], F32, name="neg_max", tag="pool0", align_bytes=64)
         row_sum = sb.tile([P, PACK], F32, name="row_sum")
-        p_exp = sb.tile([P, PACK, I], F32, name="p_exp", tag="p_exp", align_bytes=64)
+        p_exp = sb.tile([P, PACK, I], F32, name="p_exp", tag="picked0", align_bytes=64)
         for r in range(PACK):
             score = ps.tile([P, I], F32, name=f"score{r}", tag=f"bank{r}")
             cols = slice(r * P, (r + 1) * P)
@@ -179,10 +157,9 @@ def tile_attend_bvsoftened_d_pl_kernel(
                 out=score[:], lhsT=q_codes[:, cols].bitcast(FP8X4), lhsT_scale=q_scales[:, cols],
                 rhs=k_codes[:].bitcast(FP8X4), rhs_scale=k_scales[:], start=True, stop=True,
             )
-            neg_max = sb.tile([P, 1], F32, name=f"neg_max{r}", tag=f"max{r}", align_bytes=64)
-            nc.vector.tensor_reduce(neg_max[:], score[:], AXIS.X, ALU.max, negate=True)
+            nc.vector.tensor_reduce(neg_max[:, r : r + 1], score[:], AXIS.X, ALU.max, negate=True)
             nc.scalar.activation(
-                p_exp[:, r, :], score[:], ACT.Exp, bias=neg_max[:], accum_out=row_sum[:, r : r + 1]
+                p_exp[:, r, :], score[:], ACT.Exp, bias=neg_max[:, r : r + 1], accum_out=row_sum[:, r : r + 1]
             )
 
         pre_sq = sb.tile([P, HALVES], F32, name="pre_sq")
@@ -193,53 +170,54 @@ def tile_attend_bvsoftened_d_pl_kernel(
         square_up(0)
         pick(1)
         look_up(1)
-        invert(0)
-        inv_sum = sb.tile([P, PACK], F32, name="inv_sum", tag="inv_sum", align_bytes=64)
+        inv_sum = sb.tile([P, PACK], F32, name="inv_sum", tag="pool1", align_bytes=64)
         nc.vector.reciprocal(inv_sum[:], row_sum[:])
         pick(2)
-        row_factor = sb.tile([P, PACK], F32, name="row_factor")
-        nc.vector.tensor_tensor(row_factor[:], inv_sum[:], qs_col[:], ALU.mult)
+        look_up(2)
         pick(3)
-        w_bf = sb.tile([P, I, PACK], BF16, name="w_bf", align_bytes=64)
-        runs = I // PACK
-        nc.vector.tensor_tensor(
-            w_bf[:].rearrange("p (c i) r -> p c r i", i=PACK),
-            p_exp[:].rearrange("p r (c i) -> p c r i", i=PACK),
-            row_factor[:].unsqueeze(1).unsqueeze(3).to_broadcast([P, runs, PACK, PACK]),
-            ALU.mult,
-        )
-        g_bf = sb.tile([P, PACK, P, PACK], BF16, name="g_bf", tag="pool3", align_bytes=64)
-        deal(nc.vector.tensor_copy, g_bf[:, :, 0 : P // 2, :], g_raw[0][:], 0, P // 2)
+        invert(0)
+        look_up(3)
+        row_factor = sb.tile([P, PACK], F32, name="row_factor")
+        nc.gpsimd.tensor_tensor(row_factor[:], inv_sum[:], qs_col[:], ALU.mult)
+        w_bf = sb.tile([P, I, PACK], BF16, name="w_bf", tag="pool3", align_bytes=64)
         w_codes = sb.tile([P, I], U32, name="w_codes", align_bytes=64)
         w_scales = sb.tile([P, I], U8, name="w_scales", align_bytes=64)
-        nc.vector.quantize_mx(w_codes[:].bitcast(FP8X4), w_scales[:], w_bf[:].rearrange("p i r -> p (i r)"))
-        deal(nc.vector.tensor_copy, g_bf[:, :, P // 2 : P, :], g_raw[1][:], 0, P // 2)
-        look_up(2)
-        look_up(3)
-
-        g_codes = sb.tile([P, E], U32, name="g_codes", tag=PICK_AFTER[3], align_bytes=64)
-        g_scales = sb.tile([P, E], U8, name="g_scales", align_bytes=64)
-        for pair in range(2):
-            feats = slice(2 * pair * P, 2 * (pair + 1) * P)
-            nc.vector.quantize_mx(
-                g_codes[:, feats].bitcast(FP8X4), g_scales[:, feats],
-                g_bf[:, 2 * pair : 2 * pair + 2].rearrange("p r s j -> p (r s j)"),
+        halves = [slice(h * P, (h + 1) * P) for h in range(HALVES)]
+        for slots in halves:
+            nc.vector.tensor_tensor(
+                w_bf[:, slots, :].rearrange("p (c i) r -> p c r i", i=PACK),
+                p_exp[:, :, slots].rearrange("p r (c i) -> p c r i", i=PACK),
+                row_factor[:].unsqueeze(1).unsqueeze(3).to_broadcast([P, P // PACK, PACK, PACK]),
+                ALU.mult,
             )
-        all_slopes = sb.tile([P, PACK * I], F32, name="all_slopes", tag="pool3", align_bytes=64)
+        for slots in halves:
+            nc.vector.quantize_mx(
+                w_codes[:, slots].bitcast(FP8X4), w_scales[:, slots], w_bf[:, slots, :].rearrange("p i r -> p (i r)")
+            )
         slope_of(0)
         square_up(1)
         square_up(2)
         invert(1)
         invert(2)
 
-        c0 = {}
-        for g, (lo, hi) in enumerate(GROUPS):
-            c0[g] = ps.tile([P, HALVES, (hi - lo) * P], F32, name=f"c0_{g}")
-            feats = slice(lo * P, hi * P)
+        g_bf = sb.tile([P, E, PACK], BF16, name="g_bf", tag="picked0", align_bytes=64)
+        g_codes = sb.tile([P, E], U32, name="g_codes", align_bytes=64)
+        g_scales = sb.tile([P, E], U8, name="g_scales", align_bytes=64)
+        parts = [slice(0, E // 2), slice(E // 2, E)]
+        for feats in parts:
+            nc.vector.tensor_copy(
+                out=g_bf[:, feats, :].rearrange("p (c i) j -> p c j i", i=PACK),
+                in_=g_raw[:, :, feats].rearrange("p j (c i) -> p c j i", i=PACK),
+            )
+        c0 = [ps.tile([P, E], F32, name=f"c0_{h}") for h in range(HALVES)]
+        for feats in parts:
+            nc.vector.quantize_mx(
+                g_codes[:, feats].bitcast(FP8X4), g_scales[:, feats], g_bf[:, feats, :].rearrange("p e j -> p (e j)")
+            )
             for h in range(HALVES):
                 cols = slice(h * P, (h + 1) * P)
                 nc.tensor.matmul_mx(
-                    out=c0[g][:, h, :], lhsT=w_codes[:, cols].bitcast(FP8X4), lhsT_scale=w_scales[:, cols],
+                    out=c0[h][:, feats], lhsT=w_codes[:, cols].bitcast(FP8X4), lhsT_scale=w_scales[:, cols],
                     rhs=g_codes[:, feats].bitcast(FP8X4), rhs_scale=g_scales[:, feats], start=True, stop=True,
                 )
 
@@ -255,37 +233,42 @@ def tile_attend_bvsoftened_d_pl_kernel(
             dx = sb.tile([P, HALVES, n * P], F32, name=f"dx{g}")
             for h in range(HALVES):
                 nc.vector.scalar_tensor_tensor(
-                    dx[:, h, :], c0[g][:, h, :], sg_two[:, h : h + 1], slope[:, h, :], ALU.mult, ALU.mult
+                    dx[:, h, :].rearrange("p (t s) -> p t s", s=P),
+                    c0[h][:].rearrange("p (s t) -> p t s", t=PACK)[:, lo:hi, :], sg_two[:, h : h + 1],
+                    slope[:, h, :].rearrange("p (t s) -> p t s", s=P), ALU.mult, ALU.mult
                 )
             backs[g] = ps.tile([P, n, I], F32, name=f"back{g}", tag=BANKS[g])
-            for t in range(n):
-                for h in range(HALVES):
+            for h in range(HALVES):
+                for t in range(n):
                     nc.tensor.transpose(backs[g][:, t, h * P : (h + 1) * P], dx[:, h, t * P : (t + 1) * P], ident[:])
 
         def finish(g):
             lo, hi = GROUPS[g]
-            nc.vector.tensor_tensor(y[:, lo:hi, :], backs[g][:], olds[g][:], ALU.add)
+            nc.vector.tensor_tensor(y[:, lo:hi, :], backs[g][:], old_sb[:, lo:hi, :], ALU.add)
             nc.sync.dma_start(y_rows[:, lo:hi, :], y[:, lo:hi, :])
 
-        def round_columns(copy, lo, hi):
-            copy(
-                out=y_bf[:, lo:hi, :].rearrange("p (c i) t -> p c t i", i=PACK),
-                in_=y[:, :, lo:hi].rearrange("p t (c i) -> p c t i", i=PACK),
-            )
-
-        chain(0)
         slope_of(1)
         slope_of(2)
+        chain(0)
         chain(1)
-        finish(0)
         chain(2)
+        finish(0)
         finish(1)
-        finish(2)
-        round_columns(nc.vector.tensor_copy, 0, Y_SPLIT)
-        round_columns(nc.scalar.copy, Y_SPLIT, I)
+        last = PACK - 1
+        for slots in halves:
+            nc.vector.tensor_tensor(y[:, last, slots], backs[2][:, 0, slots], old_sb[:, last, slots], ALU.add)
+        nc.sync.dma_start(y_rows[:, last, :], y[:, last, :])
         y_codes = sb.tile([P, I], U32, name="y_codes", align_bytes=64)
         y_scales = sb.tile([P, I], U8, name="y_scales", align_bytes=64)
-        nc.vector.quantize_mx(y_codes[:].bitcast(FP8X4), y_scales[:], y_bf[:].rearrange("p i t -> p (i t)"))
+        for slots in halves:
+            nc.vector.tensor_copy(
+                out=y_bf[:, slots, :].rearrange("p (c i) t -> p c t i", i=PACK),
+                in_=y[:, :, slots].rearrange("p t (c i) -> p c t i", i=PACK),
+            )
+        for slots in halves:
+            nc.vector.quantize_mx(
+                y_codes[:, slots].bitcast(FP8X4), y_scales[:, slots], y_bf[:, slots, :].rearrange("p i t -> p (i t)")
+            )
         nc.sync.dma_start(out_1[0].rearrange("p c r -> p (c r)").bitcast(I32), y_codes[:].bitcast(I32))
         for quad in range(4):
             queue = nc.scalar if quad % 2 == 0 else nc.sync

@@ -20,14 +20,18 @@ AXIS = mybir.AxisListType
 P = 128
 PACK = 4
 HALVES = I // P
+QUADRANTS = 4
+ALIGN = 64
+
 GROUPS = ((0, 1), (1, 3), (3, 4))
-BANKS = ("spare", "bank0", "bank1")
+GROUP_BANKS = ("spare", "score0", "score1")
+VECTOR_QUADS = 40
 
 
-def deal(engine_copy, grouped, raw, lo, hi):
+def deal_queries(engine_copy, dealt, raw, first, end):
     engine_copy(
-        out=grouped[:, :, lo:hi, :].rearrange("p r s j -> p s j r"),
-        in_=raw.rearrange("p j (s r) -> p s j r", r=PACK)[:, lo:hi, :, :],
+        out=dealt[:, :, first:end, :].rearrange("p r s j -> p s j r"),
+        in_=raw.rearrange("p j (s r) -> p s j r", r=PACK)[:, first:end, :, :],
     )
 
 
@@ -39,122 +43,109 @@ def tile_attend_bvsoftened_d_pl_kernel(
         sb = ctx.enter_context(tc.tile_pool(name="sb", bufs=1))
         ps = ctx.enter_context(tc.psum_pool(name="ps", bufs=1))
 
-        key_bytes = sb.tile([P, T], U8, name="key_bytes", align_bytes=64)
+        key_bytes = sb.tile([P, T], U8, name="key_bytes", align_bytes=ALIGN)
         nc.vector.memset(key_bytes[:].bitcast(I32), 0)
 
         ident = sb.tile([P, P], F32, name="ident")
         make_identity(nc, ident[:])
+
+        soft_col = sb.tile([P, PACK], F32, name="soft_col")
+        nc.sync.dma_start(soft_col[:], softn.rearrange("(p t) o -> p (t o)", t=PACK))
         q_rows = query.rearrange("(p j) q -> p j q", j=PACK)
-        q_raw0 = sb.tile([P, PACK, Q // 2], F32, name="q_raw0")
-        nc.sync.dma_start(q_raw0[:], q_rows[:, :, 0 : Q // 2])
+        q_left = sb.tile([P, PACK, Q // 2], F32, name="q_left")
+        nc.sync.dma_start(q_left[:], q_rows[:, :, 0 : Q // 2])
         offsets = sb.tile([P, I // 16], U16, name="offsets")
         nc.sync.dma_start(offsets[:], offs)
-        for quad in range(4):
+        for quad in range(QUADRANTS):
             nc.sync.dma_start(
                 key_bytes[32 * quad : 32 * quad + 4, :].bitcast(I32),
                 keys_scales[0, 4 * quad : 4 * quad + 4, :].bitcast(I32),
             )
-        q_raw1 = sb.tile([P, PACK, Q // 2], F32, name="q_raw1")
-        nc.sync.dma_start(q_raw1[:], q_rows[:, :, Q // 2 : Q])
-        key_words = sb.tile([P, T], U32, name="key_words", tag="key_words", align_bytes=64)
-        nc.sync.dma_start(key_words[:].bitcast(I32), keys_words[0].rearrange("p n t -> p (n t)").bitcast(I32))
+        q_right = sb.tile([P, PACK, Q // 2], F32, name="q_right")
+        nc.sync.dma_start(q_right[:], q_rows[:, :, Q // 2 : Q])
+        key_words = sb.tile([P, T], U32, name="key_words", align_bytes=ALIGN)
+        nc.sync.dma_start(key_words[:].bitcast(I32), keys_words[0].rearrange("p n j -> p (n j)").bitcast(I32))
 
-        soft_col = sb.tile([P, PACK], F32, name="soft_col")
-        nc.sync.dma_start(soft_col[:], softn.rearrange("(p t) o -> p (t o)", t=PACK))
-        vals_rows = vals.rearrange("(p t) n -> p t n", t=PACK)
-        pools = []
-        for t in range(PACK):
-            pool_t = sb.tile([P, T], F32, name=f"pool{t}", tag=f"pool{t}", align_bytes=64)
-            nc.sync.dma_start(pool_t[:], vals_rows[:, t, :])
-            pools.append(pool_t)
-            if t == 0:
-                qs_col = sb.tile([P, PACK], F32, name="qs_col")
-                nc.sync.dma_start(qs_col[:], qs.rearrange("(p r) o -> p (r o)", r=PACK))
-                pre_col = sb.tile([P, HALVES], F32, name="pre_col")
-                sg_col = sb.tile([P, HALVES], F32, name="sg_col")
-                with nc.allow_non_contiguous_dma(reason="one value a partition"):
-                    nc.sync.dma_start(pre_col[:], pre.rearrange("o (h p) -> p (o h)", p=P))
-                    nc.sync.dma_start(sg_col[:], sg.rearrange("o (h p) -> p (o h)", p=P))
-        g_raw = sb.tile([P, PACK, E], F32, name="g_raw", tag="g_raw", align_bytes=64)
+        vals_planes = vals.rearrange("(p t) n -> p t n", t=PACK)
+        windows = []
+
+        def load_plane(t):
+            window = sb.tile([P, T], F32, name=f"window{t}", tag=f"window{t}", align_bytes=ALIGN)
+            nc.sync.dma_start(window[:], vals_planes[:, t, :])
+            windows.append(window)
+
+        load_plane(0)
+        qs_col = sb.tile([P, PACK], F32, name="qs_col")
+        nc.sync.dma_start(qs_col[:], qs.rearrange("(p r) o -> p (r o)", r=PACK))
+        pre_col = sb.tile([P, HALVES], F32, name="pre_col")
+        sg_col = sb.tile([P, HALVES], F32, name="sg_col")
+        with nc.allow_non_contiguous_dma(reason="slot 128 h + p goes to partition p, column h"):
+            nc.sync.dma_start(pre_col[:], pre.rearrange("o (h p) -> p (o h)", p=P))
+            nc.sync.dma_start(sg_col[:], sg.rearrange("o (h p) -> p (o h)", p=P))
+        for t in range(1, PACK):
+            load_plane(t)
+        g_raw = sb.tile([P, PACK, E], F32, name="g_raw", tag="g_raw", align_bytes=ALIGN)
         nc.sync.dma_start(g_raw[:], grows.rearrange("(p j) e -> p j e", j=PACK))
-        old_sb = sb.tile([P, PACK, I], F32, name="old_sb")
-        nc.sync.dma_start(old_sb[:], old.rearrange("(p t) i -> p t i", t=PACK))
+        old_planes = sb.tile([P, PACK, I], F32, name="old_planes")
+        nc.sync.dma_start(old_planes[:], old.rearrange("(p t) i -> p t i", t=PACK))
 
         root_soft = sb.tile([P, PACK], F32, name="root_soft")
-        half = sb.tile([P, PACK], F32, name="half")
-        nc.gpsimd.memset(half[:], 0.5)
-        nc.gpsimd.tensor_tensor(root_soft[:], soft_col[:], half[:], ALU.pow)
+        root_power = sb.tile([P, PACK], F32, name="root_power")
+        nc.gpsimd.memset(root_power[:], 0.5)
+        nc.gpsimd.tensor_tensor(root_soft[:], soft_col[:], root_power[:], ALU.pow)
 
-        q_bf = sb.tile([P, PACK, P, PACK], BF16, name="q_bf", align_bytes=64)
-        deal(nc.vector.tensor_copy, q_bf[:, :, 0 : P // 2, :], q_raw0[:], 0, P // 2)
-        k_scales = sb.tile([P, I], U8, name="k_scales", align_bytes=64)
+        q_bf = sb.tile([P, PACK, P, PACK], BF16, name="q_bf", align_bytes=ALIGN)
+        deal_queries(nc.vector.tensor_copy, q_bf[:, :, 0 : P // 2, :], q_left[:], 0, P // 2)
+        k_scales = sb.tile([P, I], U8, name="k_scales", align_bytes=ALIGN)
         nc.vector.tensor_copy(k_scales[:], key_bytes[:].indirect(offsets[:]))
-        deal(nc.vector.tensor_copy, q_bf[:, :, P // 2 : P, :], q_raw1[:], 0, P // 2)
-        q_codes = sb.tile([P, Q], U32, name="q_codes", align_bytes=64)
-        q_scales = sb.tile([P, Q], U8, name="q_scales", align_bytes=64)
+        deal_queries(nc.vector.tensor_copy, q_bf[:, :, P // 2 : P, :], q_right[:], 0, VECTOR_QUADS)
+        deal_queries(nc.scalar.copy, q_bf[:, :, P // 2 : P, :], q_right[:], VECTOR_QUADS, P // 2)
+        q_codes = sb.tile([P, Q], U32, name="q_codes", align_bytes=ALIGN)
+        q_scales = sb.tile([P, Q], U8, name="q_scales", align_bytes=ALIGN)
         nc.vector.quantize_mx(q_codes[:].bitcast(FP8X4), q_scales[:], q_bf[:].rearrange("p r s j -> p (r s j)"))
-        k_codes = sb.tile([P, I], U32, name="k_codes", align_bytes=64)
+        k_codes = sb.tile([P, I], U32, name="k_codes", align_bytes=ALIGN)
         nc.vector.tensor_copy(k_codes[:], key_words[:].indirect(offsets[:]))
 
-        picks = {}
+        picked, turned, s_squared, recips, turned_back = {}, {}, {}, {}, {}
 
         def pick(t):
-            picks[t] = sb.tile([P, I], F32, name=f"picked{t}", tag=f"picked{t}", align_bytes=64)
-            nc.vector.tensor_copy(picks[t][:], pools[t][:].indirect(offsets[:]))
+            picked[t] = sb.tile([P, I], F32, name=f"picked{t}", tag=f"picked{t}", align_bytes=ALIGN)
+            nc.vector.tensor_copy(picked[t][:], windows[t][:].indirect(offsets[:]))
 
-        u_banks = {}
-
-        def look_up(t):
-            g = [lo <= t < hi for lo, hi in GROUPS].index(True)
-            lo, hi = GROUPS[g]
-            if t == lo:
-                u_banks[g] = ps.tile([P, HALVES, hi - lo, P], F32, name=f"u_t{g}", tag=BANKS[g])
-            soft_sq = sb.tile([P, I], F32, name=f"soft_sq{t}", tag=f"soft_sq{t}", align_bytes=64)
-            nc.scalar.activation(soft_sq[:], picks[t][:], ACT.Square, scale=root_soft[:, t : t + 1])
+        def soften(t):
+            g = [first <= t < end for first, end in GROUPS].index(True)
+            first, end = GROUPS[g]
+            if t == first:
+                turned[g] = ps.tile([P, HALVES, end - first, P], F32, name=f"turned{g}", tag=GROUP_BANKS[g])
+            soft_sq = sb.tile([P, I], F32, name=f"soft_sq{t}", align_bytes=ALIGN)
+            nc.scalar.activation(soft_sq[:], picked[t][:], ACT.Square, scale=root_soft[:, t : t + 1])
             for h in range(HALVES):
-                nc.tensor.transpose(u_banks[g][:, h, t - lo, :], soft_sq[:, h * P : (h + 1) * P], ident[:])
+                nc.tensor.transpose(turned[g][:, h, t - first, :], soft_sq[:, h * P : (h + 1) * P], ident[:])
 
-        recips = {}
-
-        s_squares = {}
-
-        def square_up(g):
-            n = GROUPS[g][1] - GROUPS[g][0]
-            s_sq = sb.tile([P, HALVES, n * P], F32, name=f"s_sq{g}", tag=("pool0", "picked3", "s_sq2")[g], align_bytes=64)
-            s_squares[g] = s_sq
+        def square_denominator(g, tag):
+            first, end = GROUPS[g]
+            s_squared[g] = sb.tile([P, HALVES, (end - first) * P], F32, name=f"s_squared{g}", tag=tag, align_bytes=ALIGN)
             for h in range(HALVES):
                 nc.scalar.activation(
-                    s_sq[:, h, :], u_banks[g][:, h, :, :].rearrange("p t e -> p (t e)"), ACT.Square,
+                    s_squared[g][:, h, :], turned[g][:, h, :, :].rearrange("p t s -> p (t s)"), ACT.Square,
                     scale=pre_sq[:, h : h + 1], bias=1.0,
                 )
 
-        def invert(g):
-            n = GROUPS[g][1] - GROUPS[g][0]
-            s_sq = s_squares[g]
-            recips[g] = sb.tile([P, HALVES * n * P], F32, name=f"recip{g}", tag=("picked2", "soft_sq3", "recip2")[g], align_bytes=64)
-            nc.scalar.activation(recips[g][:], s_sq[:].rearrange("p h e -> p (h e)"), ACT.Abs_reciprocal_sqrt)
-
-        slopes = {}
-
-        def slope_of(g):
-            n = GROUPS[g][1] - GROUPS[g][0]
-            slopes[g] = sb.tile(
-                [P, HALVES, n * P], F32, name=f"slope{g}", tag=("slope0", "picked0", "g_raw")[g], align_bytes=64
-            )
-            nc.vector.scalar_tensor_tensor(
-                slopes[g][:].rearrange("p h e -> p (h e)"), recips[g][:], 0.5, recips[g][:], ALU.subtract, ALU.mult
-            )
+        def invert(g, tag):
+            first, end = GROUPS[g]
+            recips[g] = sb.tile([P, HALVES * (end - first) * P], F32, name=f"recip{g}", tag=tag, align_bytes=ALIGN)
+            nc.scalar.activation(recips[g][:], s_squared[g][:].rearrange("p h c -> p (h c)"), ACT.Abs_reciprocal_sqrt)
 
         pick(0)
-        look_up(0)
-        neg_max = sb.tile([P, PACK], F32, name="neg_max", tag="pool0", align_bytes=64)
+        soften(0)
+        neg_max = sb.tile([P, PACK], F32, name="neg_max", tag="window0", align_bytes=ALIGN)
         row_sum = sb.tile([P, PACK], F32, name="row_sum")
-        p_exp = sb.tile([P, PACK, I], F32, name="p_exp", tag="picked0", align_bytes=64)
+        p_exp = sb.tile([P, PACK, I], F32, name="p_exp", tag="picked0", align_bytes=ALIGN)
         for r in range(PACK):
-            score = ps.tile([P, I], F32, name=f"score{r}", tag=f"bank{r}")
-            cols = slice(r * P, (r + 1) * P)
+            score = ps.tile([P, I], F32, name=f"score{r}", tag=f"score{r}")
+            rows = slice(r * P, (r + 1) * P)
             nc.tensor.matmul_mx(
-                out=score[:], lhsT=q_codes[:, cols].bitcast(FP8X4), lhsT_scale=q_scales[:, cols],
+                out=score[:], lhsT=q_codes[:, rows].bitcast(FP8X4), lhsT_scale=q_scales[:, rows],
                 rhs=k_codes[:].bitcast(FP8X4), rhs_scale=k_scales[:], start=True, stop=True,
             )
             nc.vector.tensor_reduce(neg_max[:, r : r + 1], score[:], AXIS.X, ALU.max, negate=True)
@@ -164,113 +155,110 @@ def tile_attend_bvsoftened_d_pl_kernel(
 
         pre_sq = sb.tile([P, HALVES], F32, name="pre_sq")
         nc.scalar.activation(pre_sq[:], pre_col[:], ACT.Square)
-        sg_two = sb.tile([P, HALVES], F32, name="sg_two")
-        nc.scalar.activation(sg_two[:], sg_col[:], ACT.Copy, scale=2.0)
+        sg_twice = sb.tile([P, HALVES], F32, name="sg_twice")
+        nc.scalar.activation(sg_twice[:], sg_col[:], ACT.Copy, scale=2.0)
 
-        square_up(0)
+        square_denominator(0, tag="window0")
         pick(1)
-        look_up(1)
-        inv_sum = sb.tile([P, PACK], F32, name="inv_sum", tag="pool1", align_bytes=64)
+        soften(1)
+        inv_sum = sb.tile([P, PACK], F32, name="inv_sum", tag="window1", align_bytes=ALIGN)
         nc.vector.reciprocal(inv_sum[:], row_sum[:])
         pick(2)
-        look_up(2)
+        soften(2)
         pick(3)
-        invert(0)
-        look_up(3)
+        invert(0, tag="picked2")
+        soften(3)
+
         row_factor = sb.tile([P, PACK], F32, name="row_factor")
         nc.gpsimd.tensor_tensor(row_factor[:], inv_sum[:], qs_col[:], ALU.mult)
-        w_bf = sb.tile([P, I, PACK], BF16, name="w_bf", tag="pool3", align_bytes=64)
-        w_codes = sb.tile([P, I], U32, name="w_codes", align_bytes=64)
-        w_scales = sb.tile([P, I], U8, name="w_scales", align_bytes=64)
-        halves = [slice(h * P, (h + 1) * P) for h in range(HALVES)]
-        for slots in halves:
+        w_bf = sb.tile([P, I, PACK], BF16, name="w_bf", tag="window3", align_bytes=ALIGN)
+        w_codes = sb.tile([P, I], U32, name="w_codes", align_bytes=ALIGN)
+        w_scales = sb.tile([P, I], U8, name="w_scales", align_bytes=ALIGN)
+        slot_halves = [slice(h * P, (h + 1) * P) for h in range(HALVES)]
+        for slots in slot_halves:
             nc.vector.tensor_tensor(
-                w_bf[:, slots, :].rearrange("p (c i) r -> p c r i", i=PACK),
-                p_exp[:, :, slots].rearrange("p r (c i) -> p c r i", i=PACK),
+                w_bf[:, slots, :].rearrange("p (c n) r -> p c r n", n=PACK),
+                p_exp[:, :, slots].rearrange("p r (c n) -> p c r n", n=PACK),
                 row_factor[:].unsqueeze(1).unsqueeze(3).to_broadcast([P, P // PACK, PACK, PACK]),
                 ALU.mult,
             )
-        for slots in halves:
+        for slots in slot_halves:
             nc.vector.quantize_mx(
                 w_codes[:, slots].bitcast(FP8X4), w_scales[:, slots], w_bf[:, slots, :].rearrange("p i r -> p (i r)")
             )
-        slope_of(0)
-        square_up(1)
-        square_up(2)
-        invert(1)
-        invert(2)
 
-        g_bf = sb.tile([P, E, PACK], BF16, name="g_bf", tag="picked0", align_bytes=64)
-        g_codes = sb.tile([P, E], U32, name="g_codes", align_bytes=64)
-        g_scales = sb.tile([P, E], U8, name="g_scales", align_bytes=64)
-        parts = [slice(0, E // 2), slice(E // 2, E)]
-        for feats in parts:
+        square_denominator(1, tag="picked3")
+        invert(1, tag="recip1")
+        square_denominator(2, tag="s_squared2")
+        invert(2, tag="recip2")
+
+        g_bf = sb.tile([P, E, PACK], BF16, name="g_bf", tag="picked0", align_bytes=ALIGN)
+        g_codes = sb.tile([P, E], U32, name="g_codes", align_bytes=ALIGN)
+        g_scales = sb.tile([P, E], U8, name="g_scales", align_bytes=ALIGN)
+        feature_halves = [slice(0, E // 2), slice(E // 2, E)]
+        for feats in feature_halves:
             nc.vector.tensor_copy(
-                out=g_bf[:, feats, :].rearrange("p (c i) j -> p c j i", i=PACK),
-                in_=g_raw[:, :, feats].rearrange("p j (c i) -> p c j i", i=PACK),
+                out=g_bf[:, feats, :].rearrange("p (c n) j -> p c j n", n=PACK),
+                in_=g_raw[:, :, feats].rearrange("p j (c n) -> p c j n", n=PACK),
             )
         c0 = [ps.tile([P, E], F32, name=f"c0_{h}") for h in range(HALVES)]
-        for feats in parts:
+        for feats in feature_halves:
             nc.vector.quantize_mx(
                 g_codes[:, feats].bitcast(FP8X4), g_scales[:, feats], g_bf[:, feats, :].rearrange("p e j -> p (e j)")
             )
-            for h in range(HALVES):
-                cols = slice(h * P, (h + 1) * P)
+            for h, slots in enumerate(slot_halves):
                 nc.tensor.matmul_mx(
-                    out=c0[h][:, feats], lhsT=w_codes[:, cols].bitcast(FP8X4), lhsT_scale=w_scales[:, cols],
+                    out=c0[h][:, feats], lhsT=w_codes[:, slots].bitcast(FP8X4), lhsT_scale=w_scales[:, slots],
                     rhs=g_codes[:, feats].bitcast(FP8X4), rhs_scale=g_scales[:, feats], start=True, stop=True,
                 )
 
+        single_slopes = sb.tile([P, 2, I], F32, name="single_slopes", tag="g_raw", align_bytes=ALIGN)
+        pair_slope = sb.tile([P, 2 * I], F32, name="pair_slope", tag="picked0", align_bytes=ALIGN)
+        slopes = [single_slopes[:, 0, :], pair_slope[:], single_slopes[:, 1, :]]
         y = sb.tile([P, PACK, I], F32, name="y")
-        y_rows = out_0.rearrange("(p t) i -> p t i", t=PACK)
-        y_bf = sb.tile([P, I, PACK], BF16, name="y_bf", align_bytes=64)
-        backs = {}
+        y_planes = out_0.rearrange("(p t) i -> p t i", t=PACK)
+        y_bf = sb.tile([P, I, PACK], BF16, name="y_bf", align_bytes=ALIGN)
+        for g in range(len(GROUPS)):
+            nc.vector.scalar_tensor_tensor(slopes[g], recips[g][:], 0.5, recips[g][:], ALU.subtract, ALU.mult)
 
-        def chain(g):
-            lo, hi = GROUPS[g]
-            n = hi - lo
-            slope = slopes[g]
-            dx = sb.tile([P, HALVES, n * P], F32, name=f"dx{g}")
+        for g, (first, end) in enumerate(GROUPS):
+            planes = end - first
+            slope = slopes[g].rearrange("p (h c) -> p h c", h=HALVES)
+            gained = sb.tile([P, HALVES, planes * P], F32, name=f"gained{g}")
             for h in range(HALVES):
                 nc.vector.scalar_tensor_tensor(
-                    dx[:, h, :].rearrange("p (t s) -> p t s", s=P),
-                    c0[h][:].rearrange("p (s t) -> p t s", t=PACK)[:, lo:hi, :], sg_two[:, h : h + 1],
-                    slope[:, h, :].rearrange("p (t s) -> p t s", s=P), ALU.mult, ALU.mult
+                    gained[:, h, :].rearrange("p (t s) -> p t s", s=P),
+                    c0[h][:].rearrange("p (s t) -> p t s", t=PACK)[:, first:end, :], sg_twice[:, h : h + 1],
+                    slope[:, h, :].rearrange("p (t s) -> p t s", s=P), ALU.mult, ALU.mult,
                 )
-            backs[g] = ps.tile([P, n, I], F32, name=f"back{g}", tag=BANKS[g])
-            for h in range(HALVES):
-                for t in range(n):
-                    nc.tensor.transpose(backs[g][:, t, h * P : (h + 1) * P], dx[:, h, t * P : (t + 1) * P], ident[:])
+            turned_back[g] = ps.tile([P, planes, I], F32, name=f"turned_back{g}", tag=GROUP_BANKS[g])
+            for h, slots in enumerate(slot_halves):
+                for t in range(planes):
+                    nc.tensor.transpose(turned_back[g][:, t, slots], gained[:, h, t * P : (t + 1) * P], ident[:])
 
-        def finish(g):
-            lo, hi = GROUPS[g]
-            nc.vector.tensor_tensor(y[:, lo:hi, :], backs[g][:], old_sb[:, lo:hi, :], ALU.add)
-            nc.sync.dma_start(y_rows[:, lo:hi, :], y[:, lo:hi, :])
-
-        slope_of(1)
-        slope_of(2)
-        chain(0)
-        chain(1)
-        chain(2)
-        finish(0)
-        finish(1)
-        last = PACK - 1
-        for slots in halves:
-            nc.vector.tensor_tensor(y[:, last, slots], backs[2][:, 0, slots], old_sb[:, last, slots], ALU.add)
-        nc.sync.dma_start(y_rows[:, last, :], y[:, last, :])
-        y_codes = sb.tile([P, I], U32, name="y_codes", align_bytes=64)
-        y_scales = sb.tile([P, I], U8, name="y_scales", align_bytes=64)
-        for slots in halves:
-            nc.vector.tensor_copy(
-                out=y_bf[:, slots, :].rearrange("p (c i) t -> p c t i", i=PACK),
-                in_=y[:, :, slots].rearrange("p t (c i) -> p c t i", i=PACK),
+        for g, (first, end) in enumerate(GROUPS[:-1]):
+            nc.vector.tensor_tensor(y[:, first:end, :], turned_back[g][:], old_planes[:, first:end, :], ALU.add)
+            nc.sync.dma_start(y_planes[:, first:end, :], y[:, first:end, :])
+        last_group, last_plane = len(GROUPS) - 1, PACK - 1
+        for slots in slot_halves:
+            nc.vector.tensor_tensor(
+                y[:, last_plane, slots], turned_back[last_group][:, 0, slots], old_planes[:, last_plane, slots], ALU.add
             )
-        for slots in halves:
+        nc.sync.dma_start(y_planes[:, last_plane, :], y[:, last_plane, :])
+
+        y_codes = sb.tile([P, I], U32, name="y_codes", align_bytes=ALIGN)
+        y_scales = sb.tile([P, I], U8, name="y_scales", align_bytes=ALIGN)
+        for slots in slot_halves:
+            nc.vector.tensor_copy(
+                out=y_bf[:, slots, :].rearrange("p (c n) t -> p c t n", n=PACK),
+                in_=y[:, :, slots].rearrange("p t (c n) -> p c t n", n=PACK),
+            )
+        for slots in slot_halves:
             nc.vector.quantize_mx(
                 y_codes[:, slots].bitcast(FP8X4), y_scales[:, slots], y_bf[:, slots, :].rearrange("p i t -> p (i t)")
             )
-        nc.sync.dma_start(out_1[0].rearrange("p c r -> p (c r)").bitcast(I32), y_codes[:].bitcast(I32))
-        for quad in range(4):
+        nc.sync.dma_start(out_1[0].rearrange("p i t -> p (i t)").bitcast(I32), y_codes[:].bitcast(I32))
+        for quad in range(QUADRANTS):
             queue = nc.scalar if quad % 2 == 0 else nc.sync
             queue.dma_start(
                 out_2[0, 4 * quad : 4 * quad + 4, :].bitcast(I32),

from contextlib import ExitStack

import concourse.mybir as mybir
from concourse.masks import make_identity

D, E, T, I, Q = 512, 512, 1024, 256, 512
FLOPS = 2 * D * Q * I + 2 * Q * E * I

F32 = mybir.dt.float32
BF16 = mybir.dt.bfloat16
I32 = mybir.dt.int32
U32 = mybir.dt.uint32
U16 = mybir.dt.uint16
U8 = mybir.dt.uint8
FP8X4 = mybir.dt.float8_e4m3fn_x4
ALU = mybir.AluOpType
ACT = mybir.ActivationFunctionType
AXIS = mybir.AxisListType

P = 128
PACK = 4
HALVES = I // P
QUADRANTS = 4
ALIGN = 64

GROUPS = ((0, 1), (1, 3), (3, 4))
GROUP_BANKS = ("spare", "score0", "score1")
VECTOR_QUADS = 40


def deal_queries(engine_copy, dealt, raw, first, end):
    engine_copy(
        out=dealt[:, :, first:end, :].rearrange("p r s j -> p s j r"),
        in_=raw.rearrange("p j (s r) -> p s j r", r=PACK)[:, first:end, :, :],
    )


def tile_attend_bvsoftened_d_pl_kernel(
    tc, query, qs, grows, vals, keys_words, keys_scales, softn, pre, sg, old, offs, out_0, out_1, out_2
):
    nc = tc.nc
    with ExitStack() as ctx:
        sb = ctx.enter_context(tc.tile_pool(name="sb", bufs=1))
        ps = ctx.enter_context(tc.psum_pool(name="ps", bufs=1))

        key_bytes = sb.tile([P, T], U8, name="key_bytes", align_bytes=ALIGN)
        nc.vector.memset(key_bytes[:].bitcast(I32), 0)

        ident = sb.tile([P, P], F32, name="ident")
        make_identity(nc, ident[:])

        soft_col = sb.tile([P, PACK], F32, name="soft_col")
        nc.sync.dma_start(soft_col[:], softn.rearrange("(p t) o -> p (t o)", t=PACK))
        q_rows = query.rearrange("(p j) q -> p j q", j=PACK)
        q_left = sb.tile([P, PACK, Q // 2], F32, name="q_left")
        nc.sync.dma_start(q_left[:], q_rows[:, :, 0 : Q // 2])
        offsets = sb.tile([P, I // 16], U16, name="offsets")
        nc.sync.dma_start(offsets[:], offs)
        for quad in range(QUADRANTS):
            nc.sync.dma_start(
                key_bytes[32 * quad : 32 * quad + 4, :].bitcast(I32),
                keys_scales[0, 4 * quad : 4 * quad + 4, :].bitcast(I32),
            )
        q_right = sb.tile([P, PACK, Q // 2], F32, name="q_right")
        nc.sync.dma_start(q_right[:], q_rows[:, :, Q // 2 : Q])
        key_words = sb.tile([P, T], U32, name="key_words", align_bytes=ALIGN)
        nc.sync.dma_start(key_words[:].bitcast(I32), keys_words[0].rearrange("p n j -> p (n j)").bitcast(I32))

        vals_planes = vals.rearrange("(p t) n -> p t n", t=PACK)
        windows = []

        def load_plane(t):
            window = sb.tile([P, T], F32, name=f"window{t}", tag=f"window{t}", align_bytes=ALIGN)
            nc.sync.dma_start(window[:], vals_planes[:, t, :])
            windows.append(window)

        load_plane(0)
        qs_col = sb.tile([P, PACK], F32, name="qs_col")
        nc.sync.dma_start(qs_col[:], qs.rearrange("(p r) o -> p (r o)", r=PACK))
        pre_col = sb.tile([P, HALVES], F32, name="pre_col")
        sg_col = sb.tile([P, HALVES], F32, name="sg_col")
        with nc.allow_non_contiguous_dma(reason="slot 128 h + p goes to partition p, column h"):
            nc.sync.dma_start(pre_col[:], pre.rearrange("o (h p) -> p (o h)", p=P))
            nc.sync.dma_start(sg_col[:], sg.rearrange("o (h p) -> p (o h)", p=P))
        for t in range(1, PACK):
            load_plane(t)
        g_raw = sb.tile([P, PACK, E], F32, name="g_raw", tag="g_raw", align_bytes=ALIGN)
        nc.sync.dma_start(g_raw[:], grows.rearrange("(p j) e -> p j e", j=PACK))
        old_planes = sb.tile([P, PACK, I], F32, name="old_planes")
        nc.sync.dma_start(old_planes[:], old.rearrange("(p t) i -> p t i", t=PACK))

        root_soft = sb.tile([P, PACK], F32, name="root_soft")
        root_power = sb.tile([P, PACK], F32, name="root_power")
        nc.gpsimd.memset(root_power[:], 0.5)
        nc.gpsimd.tensor_tensor(root_soft[:], soft_col[:], root_power[:], ALU.pow)

        q_bf = sb.tile([P, PACK, P, PACK], BF16, name="q_bf", align_bytes=ALIGN)
        deal_queries(nc.vector.tensor_copy, q_bf[:, :, 0 : P // 2, :], q_left[:], 0, P // 2)
        k_scales = sb.tile([P, I], U8, name="k_scales", align_bytes=ALIGN)
        nc.vector.tensor_copy(k_scales[:], key_bytes[:].indirect(offsets[:]))
        deal_queries(nc.vector.tensor_copy, q_bf[:, :, P // 2 : P, :], q_right[:], 0, VECTOR_QUADS)
        deal_queries(nc.scalar.copy, q_bf[:, :, P // 2 : P, :], q_right[:], VECTOR_QUADS, P // 2)
        q_codes = sb.tile([P, Q], U32, name="q_codes", align_bytes=ALIGN)
        q_scales = sb.tile([P, Q], U8, name="q_scales", align_bytes=ALIGN)
        nc.vector.quantize_mx(q_codes[:].bitcast(FP8X4), q_scales[:], q_bf[:].rearrange("p r s j -> p (r s j)"))
        k_codes = sb.tile([P, I], U32, name="k_codes", align_bytes=ALIGN)
        nc.vector.tensor_copy(k_codes[:], key_words[:].indirect(offsets[:]))

        picked, turned, s_squared, recips, turned_back = {}, {}, {}, {}, {}

        def pick(t):
            picked[t] = sb.tile([P, I], F32, name=f"picked{t}", tag=f"picked{t}", align_bytes=ALIGN)
            nc.vector.tensor_copy(picked[t][:], windows[t][:].indirect(offsets[:]))

        def soften(t):
            g = [first <= t < end for first, end in GROUPS].index(True)
            first, end = GROUPS[g]
            if t == first:
                turned[g] = ps.tile([P, HALVES, end - first, P], F32, name=f"turned{g}", tag=GROUP_BANKS[g])
            soft_sq = sb.tile([P, I], F32, name=f"soft_sq{t}", align_bytes=ALIGN)
            nc.scalar.activation(soft_sq[:], picked[t][:], ACT.Square, scale=root_soft[:, t : t + 1])
            for h in range(HALVES):
                nc.tensor.transpose(turned[g][:, h, t - first, :], soft_sq[:, h * P : (h + 1) * P], ident[:])

        def square_denominator(g, tag):
            first, end = GROUPS[g]
            s_squared[g] = sb.tile([P, HALVES, (end - first) * P], F32, name=f"s_squared{g}", tag=tag, align_bytes=ALIGN)
            for h in range(HALVES):
                nc.scalar.activation(
                    s_squared[g][:, h, :], turned[g][:, h, :, :].rearrange("p t s -> p (t s)"), ACT.Square,
                    scale=pre_sq[:, h : h + 1], bias=1.0,
                )

        def invert(g, tag):
            first, end = GROUPS[g]
            recips[g] = sb.tile([P, HALVES * (end - first) * P], F32, name=f"recip{g}", tag=tag, align_bytes=ALIGN)
            nc.scalar.activation(recips[g][:], s_squared[g][:].rearrange("p h c -> p (h c)"), ACT.Abs_reciprocal_sqrt)

        pick(0)
        soften(0)
        neg_max = sb.tile([P, PACK], F32, name="neg_max", tag="window0", align_bytes=ALIGN)
        row_sum = sb.tile([P, PACK], F32, name="row_sum")
        p_exp = sb.tile([P, PACK, I], F32, name="p_exp", tag="picked0", align_bytes=ALIGN)
        for r in range(PACK):
            score = ps.tile([P, I], F32, name=f"score{r}", tag=f"score{r}")
            rows = slice(r * P, (r + 1) * P)
            nc.tensor.matmul_mx(
                out=score[:], lhsT=q_codes[:, rows].bitcast(FP8X4), lhsT_scale=q_scales[:, rows],
                rhs=k_codes[:].bitcast(FP8X4), rhs_scale=k_scales[:], start=True, stop=True,
            )
            nc.vector.tensor_reduce(neg_max[:, r : r + 1], score[:], AXIS.X, ALU.max, negate=True)
            nc.scalar.activation(
                p_exp[:, r, :], score[:], ACT.Exp, bias=neg_max[:, r : r + 1], accum_out=row_sum[:, r : r + 1]
            )

        pre_sq = sb.tile([P, HALVES], F32, name="pre_sq")
        nc.scalar.activation(pre_sq[:], pre_col[:], ACT.Square)
        sg_twice = sb.tile([P, HALVES], F32, name="sg_twice")
        nc.scalar.activation(sg_twice[:], sg_col[:], ACT.Copy, scale=2.0)

        square_denominator(0, tag="window0")
        pick(1)
        soften(1)
        inv_sum = sb.tile([P, PACK], F32, name="inv_sum", tag="window1", align_bytes=ALIGN)
        nc.vector.reciprocal(inv_sum[:], row_sum[:])
        pick(2)
        soften(2)
        pick(3)
        invert(0, tag="picked2")
        soften(3)

        row_factor = sb.tile([P, PACK], F32, name="row_factor")
        nc.gpsimd.tensor_tensor(row_factor[:], inv_sum[:], qs_col[:], ALU.mult)
        w_bf = sb.tile([P, I, PACK], BF16, name="w_bf", tag="window3", align_bytes=ALIGN)
        w_codes = sb.tile([P, I], U32, name="w_codes", align_bytes=ALIGN)
        w_scales = sb.tile([P, I], U8, name="w_scales", align_bytes=ALIGN)
        slot_halves = [slice(h * P, (h + 1) * P) for h in range(HALVES)]
        for slots in slot_halves:
            nc.vector.tensor_tensor(
                w_bf[:, slots, :].rearrange("p (c n) r -> p c r n", n=PACK),
                p_exp[:, :, slots].rearrange("p r (c n) -> p c r n", n=PACK),
                row_factor[:].unsqueeze(1).unsqueeze(3).to_broadcast([P, P // PACK, PACK, PACK]),
                ALU.mult,
            )
        for slots in slot_halves:
            nc.vector.quantize_mx(
                w_codes[:, slots].bitcast(FP8X4), w_scales[:, slots], w_bf[:, slots, :].rearrange("p i r -> p (i r)")
            )

        square_denominator(1, tag="picked3")
        invert(1, tag="recip1")
        square_denominator(2, tag="s_squared2")
        invert(2, tag="recip2")

        g_bf = sb.tile([P, E, PACK], BF16, name="g_bf", tag="picked0", align_bytes=ALIGN)
        g_codes = sb.tile([P, E], U32, name="g_codes", align_bytes=ALIGN)
        g_scales = sb.tile([P, E], U8, name="g_scales", align_bytes=ALIGN)
        feature_halves = [slice(0, E // 2), slice(E // 2, E)]
        for feats in feature_halves:
            nc.vector.tensor_copy(
                out=g_bf[:, feats, :].rearrange("p (c n) j -> p c j n", n=PACK),
                in_=g_raw[:, :, feats].rearrange("p j (c n) -> p c j n", n=PACK),
            )
        c0 = [ps.tile([P, E], F32, name=f"c0_{h}") for h in range(HALVES)]
        for feats in feature_halves:
            nc.vector.quantize_mx(
                g_codes[:, feats].bitcast(FP8X4), g_scales[:, feats], g_bf[:, feats, :].rearrange("p e j -> p (e j)")
            )
            for h, slots in enumerate(slot_halves):
                nc.tensor.matmul_mx(
                    out=c0[h][:, feats], lhsT=w_codes[:, slots].bitcast(FP8X4), lhsT_scale=w_scales[:, slots],
                    rhs=g_codes[:, feats].bitcast(FP8X4), rhs_scale=g_scales[:, feats], start=True, stop=True,
                )

        single_slopes = sb.tile([P, 2, I], F32, name="single_slopes", tag="g_raw", align_bytes=ALIGN)
        pair_slope = sb.tile([P, 2 * I], F32, name="pair_slope", tag="picked0", align_bytes=ALIGN)
        slopes = [single_slopes[:, 0, :], pair_slope[:], single_slopes[:, 1, :]]
        y = sb.tile([P, PACK, I], F32, name="y")
        y_planes = out_0.rearrange("(p t) i -> p t i", t=PACK)
        y_bf = sb.tile([P, I, PACK], BF16, name="y_bf", align_bytes=ALIGN)
        for g in range(len(GROUPS)):
            nc.vector.scalar_tensor_tensor(slopes[g], recips[g][:], 0.5, recips[g][:], ALU.subtract, ALU.mult)

        for g, (first, end) in enumerate(GROUPS):
            planes = end - first
            slope = slopes[g].rearrange("p (h c) -> p h c", h=HALVES)
            gained = sb.tile([P, HALVES, planes * P], F32, name=f"gained{g}")
            for h in range(HALVES):
                nc.vector.scalar_tensor_tensor(
                    gained[:, h, :].rearrange("p (t s) -> p t s", s=P),
                    c0[h][:].rearrange("p (s t) -> p t s", t=PACK)[:, first:end, :], sg_twice[:, h : h + 1],
                    slope[:, h, :].rearrange("p (t s) -> p t s", s=P), ALU.mult, ALU.mult,
                )
            turned_back[g] = ps.tile([P, planes, I], F32, name=f"turned_back{g}", tag=GROUP_BANKS[g])
            for h, slots in enumerate(slot_halves):
                for t in range(planes):
                    nc.tensor.transpose(turned_back[g][:, t, slots], gained[:, h, t * P : (t + 1) * P], ident[:])

        for g, (first, end) in enumerate(GROUPS[:-1]):
            nc.vector.tensor_tensor(y[:, first:end, :], turned_back[g][:], old_planes[:, first:end, :], ALU.add)
            nc.sync.dma_start(y_planes[:, first:end, :], y[:, first:end, :])
        last_group, last_plane = len(GROUPS) - 1, PACK - 1
        for slots in slot_halves:
            nc.vector.tensor_tensor(
                y[:, last_plane, slots], turned_back[last_group][:, 0, slots], old_planes[:, last_plane, slots], ALU.add
            )
        nc.sync.dma_start(y_planes[:, last_plane, :], y[:, last_plane, :])

        y_codes = sb.tile([P, I], U32, name="y_codes", align_bytes=ALIGN)
        y_scales = sb.tile([P, I], U8, name="y_scales", align_bytes=ALIGN)
        for slots in slot_halves:
            nc.vector.tensor_copy(
                out=y_bf[:, slots, :].rearrange("p (c n) t -> p c t n", n=PACK),
                in_=y[:, :, slots].rearrange("p t (c n) -> p c t n", n=PACK),
            )
        for slots in slot_halves:
            nc.vector.quantize_mx(
                y_codes[:, slots].bitcast(FP8X4), y_scales[:, slots], y_bf[:, slots, :].rearrange("p i t -> p (i t)")
            )
        nc.sync.dma_start(out_1[0].rearrange("p i t -> p (i t)").bitcast(I32), y_codes[:].bitcast(I32))
        for quad in range(QUADRANTS):
            queue = nc.scalar if quad % 2 == 0 else nc.sync
            queue.dma_start(
                out_2[0, 4 * quad : 4 * quad + 4, :].bitcast(I32),
                y_scales[32 * quad : 32 * quad + 4, :].bitcast(I32),
            )
